import numpy as np, ml_dtypes
CORES = [35,38,43,46]
N = 4
BF = ml_dtypes.bfloat16
def f(rng, *shape):
    return (rng.standard_normal(shape, dtype=np.float32) * np.exp2(rng.integers(-2, 3, shape[:-1] + (1,)))).astype(BF)
def wide(rng, *shape):
    v = f(rng, *shape).astype(np.float32); k = shape[:-2] + (1, shape[-1])
    return (v * np.exp2(rng.integers(-6, 7, k)) * (rng.random(k) > 0.0625)).astype(BF)
def gentries(a):
    return np.ascontiguousarray(a.reshape(8, 16, -1).transpose(0, 2, 1)).reshape(8, -1)
def gtable(e):
    e = np.asarray(e); return np.ascontiguousarray(e.reshape(8, -1, 16).transpose(0, 2, 1)).reshape(128, -1).astype(np.int32)
E, D, CAP, S, P = 2048, 4, 512, 3, 4096
def setup_inputs(rng):
    mp = rng.integers(0, 8, (8, S)); mp[:, S - 1] = rng.permutation(8); i, j = rng.permutation(8)[:2]; mp[j, :S - 1] = mp[i, :S - 1]
    sh = (N, 8, D * E); pl = np.where(rng.random(sh) < 0.5, rng.integers(0, E, sh), rng.integers(E, P, sh)); se = rng.integers(0, E, (N, 8, N * CAP))
    return {"x": f(rng, N, 16, E), "mp": np.repeat(mp[None], N, 0).astype(np.int32),
            "src": np.stack([gtable(e) for e in pl]), "snd": np.stack([gtable(e) for e in se]),
            "bs": f(rng, N, 128, 1).astype(np.float32) * np.float32(0.25),
            "aw": rng.standard_normal((N, 16, 16), dtype=np.float32) * np.float32(0.5),
            "ab": rng.standard_normal((N, 16, 1), dtype=np.float32) * np.float32(0.25),
            "aq": np.clip(0.4 * rng.standard_normal((N, 16, 1)), -1, 1).astype(np.float32)}
def setup_inputs_full(rng):
    d = setup_inputs(rng)
    d["src"] = np.stack([gtable(np.stack([E + rng.permutation(D * E) % (N * CAP) for k in range(8)])) for r in range(N)])
    d["snd"] = np.stack([gtable(np.stack([np.concatenate([rng.permutation(E)[:CAP] for q in range(N)]) for k in range(8)])) for r in range(N)]); return d
def setup_inputs_edges(rng):
    d = setup_inputs(rng); ends = np.array([0, E - 1] + [E + q * CAP + i for q in range(N) for i in (0, CAP - 1)])
    pl = rng.choice(ends, (N, 8, D * E)); pl[:, rng.integers(0, 8)] = P - 1; se = rng.choice(np.array([0, E - 1]), (N, 8, N * CAP))
    d["src"] = np.stack([gtable(e) for e in pl]); d["snd"] = np.stack([gtable(e) for e in se]); return d
def setup_inputs_chains(rng):
    d = setup_inputs(rng); c = rng.choice(np.array([0, 7]), (3, S)); c[1, 0] = 0; c[2, 0] = 7; c[:, S - 1] = rng.permutation(8)[:3]; c[0] = c[0, S - 1]
    d["mp"] = np.repeat(c[rng.permutation(np.array([0, 0, 0, 1, 1, 2, 2, 2]))][None], N, 0).astype(np.int32); return d
def setup_inputs_dead(rng):
    d = setup_inputs(rng); k, z = rng.permutation(8)[:2]; d["bs"][:, 16 * k:16 * k + 16] = -4096; d["bs"][:, 16 * z:16 * z + 16] = 0
    g = int(np.flatnonzero(d["mp"][0, :, S - 1] != k)[rng.integers(0, 7)]); d["mp"][:, g, 0] = k; return d
def setup_inputs_spread(rng):
    d = setup_inputs(rng); d["x"] = wide(rng, N, 16, E); return d
def check_inputs(d):
    bad = []
    for a, n in (("src", P), ("snd", E), ("mp", 8)):
        if d[a].min() < 0 or d[a].max() >= n: bad.append("range of " + a)
    if (d["mp"] != d["mp"][:1]).any(): bad.append("mp is the same on all ranks")
    if not (np.abs(d["aq"]) <= 1).all(): bad.append("range of aq")
    for a in ("x", "bs", "aw", "ab", "aq"):
        if not np.isfinite(d[a].astype(np.float32)).all(): bad.append("finite " + a)
    return bad
def reference(x, mp, src, snd, bs, aw, ab, aq):
    h = np.repeat(x.astype(np.float64)[:, None], 8, axis=1)
    pl = np.stack([gentries(a) for a in src]); se = np.stack([gentries(a) for a in snd]).reshape(N, 8, N, CAP); b = bs.astype(np.float64).reshape(N, 8, 16, 1)
    for s in range(S):
        nh = np.zeros_like(h)
        for g in range(8):
            k = int(mp[0, g, s])
            for r in range(N):
                win = np.concatenate([h[r, g]] + [h[q, g][:, se[q, k, r]] for q in range(N)], axis=1)
                v = np.sum(win[:, pl[r, k]].reshape(16, D, E), axis=1)
                nh[r, g] = np.maximum(v * 2.0 ** -2 + b[r, k], 0)
        h = nh
    tot = np.zeros(8, np.float64)
    for r in range(N):
        for g in range(8):
            t = np.tanh(aw[r].astype(np.float64).T @ h[r, g] + ab[r].astype(np.float64))
            tot[g] += np.sum(aq[r].astype(np.float64) * t)
    w = np.exp(tot * 2.0 ** -13)
    y = np.einsum("g,rgce->rce", w, h)
    return {"y": y.astype(np.float32), "w": np.repeat(w[None, :, None], N, axis=0).astype(np.float32)}

@@ -1,0 +1,352 @@
+from concourse.bass import DstId, RemoteDMATransfer
+from concourse.mybir import AluOpType, AxisListType, ActivationFunctionType
+
+E, CAP, P, S = 2048, 512, 4096, 3
+F32, BF, I32, U16 = "float32", "bfloat16", "int32", "uint16"
+
+SCRATCH = {
+    "win0": ("sbuf", [128, P], BF), "win1": ("sbuf", [128, P], F32), "win2": ("sbuf", [128, P], F32),
+    "hfin": ("sbuf", [128, 16, 4, 32], F32),
+    "sb0": ("sbuf", [128, 3 * CAP], BF), "sb1": ("sbuf", [128, 3 * CAP], F32), "sb2": ("sbuf", [128, 3 * CAP], F32),
+    "acc0": ("sbuf", [128, E], F32), "acc1": ("sbuf", [128, E], F32), "acc2": ("sbuf", [128, E], F32),
+    "cg0": ("sbuf", [128, 4 * 768], BF), "cg1": ("sbuf", [128, 4 * 768], F32), "cg2": ("sbuf", [128, 4 * 768], F32),
+    "srci": ("sbuf", [128, 512], I32), "sndi": ("sbuf", [128, 128], I32),
+    "srcf": ("sbuf", [128, 512], F32), "sndf": ("sbuf", [128, 128], F32),
+    "src0": ("sbuf", [128, 512], U16), "src1": ("sbuf", [128, 512], U16), "src2": ("sbuf", [128, 512], U16),
+    "snd0": ("sbuf", [128, 128], U16), "snd12": ("sbuf", [128, 256], U16),
+    "bsb": ("sbuf", [128, 4], F32), "bias4": ("sbuf", [128, 4], F32), "bias1": ("sbuf", [128, 4], F32),
+    "mp1": ("sbuf", [1, 24], I32), "mpb": ("sbuf", [128, 24], I32),
+    "moi": ("sbuf", [128, 24], I32), "mou": ("sbuf", [128, 24], U16),
+    "dif": ("sbuf", [128, 128], F32), "difq": ("sbuf", [128, 128], F32), "pmat": ("sbuf", [128, 384], F32),
+    "ones": ("sbuf", [128, 128], F32), "idn": ("sbuf", [128, 128], F32), "idb": ("sbuf", [128, 128], BF),
+    "pi": ("sbuf", [128, 4], I32), "pg": ("sbuf", [128, 4], I32), "pgf": ("sbuf", [128, 4], F32),
+    "blk": ("sbuf", [128, 128], F32), "qm": ("sbuf", [128, 512], F32), "m16": ("sbuf", [128, 16], F32),
+    "abd": ("sbuf", [128, 128], F32), "abc": ("sbuf", [128, 4], F32), "aqc": ("sbuf", [128, 4], F32),
+    "aqs": ("sbuf", [128, 4], F32),
+    "aqd": ("dram", [128, 2], F32), "aqin": ("dram", [4, 128, 2], F32),
+    "tnh": ("sbuf", [128, E], F32), "tsum": ("sbuf", [128, 8], F32),
+    "sin": ("sbuf", [128, 8], F32), "exo": ("sbuf", [128, 4], F32), "exr": ("sbuf", [128, 4], F32),
+    "mx": ("sbuf", [128, 16], F32), "wm": ("sbuf", [128, 16], F32),
+    "yo": ("sbuf", [128, 256], F32),
+}
+for _b in range(8):
+    SCRATCH["ps%d" % _b] = ("psum", [128, 512], F32)
+
+SEMAPHORES = ["cv", "ca", "cp", "cg", "lx", "lsnd", "lsrc", "lmp", "lbs", "lpar", "laq", "sent",
+              "arr0", "arr1", "arr2", "arrq", "arrn", "arrf", "ow", "oy"]
+
+CHUNKS = [
+    [("D", 256), ("A", 512), ("A", 320), ("A", 256), ("C", 512), ("C", 192)],
+    [("D", 256), ("A", 512), ("A", 384), ("A", 256), ("C", 512), ("C", 128)],
+    [("D", 256), ("A", 256), ("A", 512), ("A", 512), ("A", 128), ("C", 384)],
+]
+ORD = {
+    "v0": "0.0 0.1 1.1 0.2 3.1 1.2 2.1 0.3 2.2 3.2 1.3 2.3 3.3".split(),
+    "a0": "1.0 3.0 4.0 2.0 4.1 4.2 4.3 5.0 5.1 5.2 5.3 r4 r5".split(),
+    "p0": "c4.0 c4.1 c4.2 c4.3 c5.0 c5.1 c5.2 c5.3".split(),
+    "v1": "0.0 0.1 0.2 3.1 0.3 3.2 2.1 3.3 2.2 1.1 2.3 1.2 1.3".split(),
+    "a1": "4.0 3.0 4.1 2.0 4.2 1.0 5.0 5.1 4.3 5.2 5.3 r4 r5".split(),
+    "p1": "c4.0 c4.1 c4.2 c5.0 c5.1 c4.3 c5.2 c5.3".split(),
+    "v2": "0.0 0.1 2.1 0.2 2.2 0.3 3.1 2.3 3.2 4.1 3.3 1.1 r3 1.2 4.2 1.3 r1 4.3 r4".split(),
+    "a2": "2.0 5.0 5.1 3.0 5.2 5.3 r0 4.0 1.0 r2 r5 t0 t2 t5 t3 t1 t4".split(),
+    "p2": "c5.0 c5.1 c5.2 c5.3 m0 m2 m5 m3 m1 m4".split(),
+}
+
+
+def rank_program(g, core, T, topo):
+    rank = T.rank_of(core)
+    if rank is None:
+        return
+    A, F = AluOpType, ActivationFunctionType
+    V, SC, PE, SY = g.vector, g.scalar, g.tensor, g.sync
+    eng = {"v": V, "a": SC, "p": PE, "g": g, "s": SY}
+    cores = list(T.cores)
+    near = [q for q in range(len(cores)) if q != rank and topo.chip(cores[q]) == topo.chip(core)]
+    far = [q for q in range(len(cores)) if topo.chip(cores[q]) != topo.chip(core)]
+    far.sort(key=lambda q: topo.die(cores[q]) == topo.die(core))
+    peers = far + near
+    off_eng = topo.engines(core, cores[far[0]])
+    on_eng = [e for e in topo.engines(core, cores[near[0]]) if e not in off_eng]
+    off_mask, on_mask = sum(1 << e for e in off_eng), sum(1 << e for e in on_eng)
+    share = len(off_eng) // len(far)
+    small_masks = [sum(1 << e for e in off_eng[i * share:(i + 1) * share]) for i in range(len(far))] + [on_mask]
+    n_slots = len(far) * len(off_eng) + len(on_eng)
+    n_small = share * len(far) + len(on_eng)
+
+    def dst(q):
+        rid, pid, _ = topo.addr(cores[q])
+        return DstId(rid=rid, pnc=pid)
+
+    ops, order = {}, {q: [] for q in eng}
+    tok = {"arr0": ("arr0", n_slots), "arr1": ("arr1", n_slots), "arr2": ("arr2", n_slots), "arrq": ("arrq", n_small),
+           "arrn": ("arrn", len(on_eng)), "arrf": ("arrf", share * len(far))}
+    dmas = {}
+
+    def op(name, deps, fn):
+        ops[name] = (deps, fn, None)
+
+    def dma(name, sem, deps, fn):
+        ops[name] = (deps, fn, sem)
+        dmas[sem] = dmas.get(sem, 0) + 16
+
+    def remote(name, deps, fn):
+        ops[name] = (deps, fn, "remote")
+
+    def put(q, *names):
+        order[q].extend(names)
+
+    def gather(q, out, win, off, bias=None, relu=False):
+        src = win.indirect(off)
+        if relu:
+            return finish(q, out, src)
+        if q == "a":
+            if bias is None:
+                return SC.activation(out, src, F.Copy)
+            return SC.activation(out, src, F.Identity, bias=bias)
+        if bias is None:
+            return V.tensor_copy(out, src)
+        return V.tensor_scalar(out, src, bias, None, A.add)
+
+    def finish(q, out, total):
+        if q == "a":
+            return SC.activation(out, total, F.Relu, scale=0.25)
+        return V.tensor_scalar(out, total, 0.25, 0.0, A.mult, A.max)
+
+    ps = [T["ps%d" % b] for b in range(8)]
+    win = [T.win0, T.win1, T.win2]
+    sb = [T.sb0, T.sb1, T.sb2]
+    srcu = [T.src0, T.src1, T.src2]
+    acc = [T.acc0, T.acc1, T.acc2]
+    cgb = [T.cg0, T.cg1, T.cg2]
+
+    for k in range(8):
+        dma("x%d" % k, "lx", [], lambda k=k, q=(SY if k < 4 else SC): q.dma_start(T.win0[16 * k:16 * k + 16, 0:E], T.x[:]))
+    dma("snd", "lsnd", [], lambda: SY.dma_start(T.sndi[:], T.snd[:]))
+    dma("mp", "lmp", [], lambda: SC.dma_start(T.mp1[:], T.mp[:]))
+    dma("src", "lsrc", [], lambda: SY.dma_start(T.srci[:], T.src[:]))
+    dma("bs", "lbs", [], lambda: SC.dma_start(T.bsb[:, 0:1], T.bs[:]))
+    dma("aqd", "laq", [], lambda: SY.dma_start(T.aqd[0:8, :], T.aq[:]))
+    dma("aqf", "laq", [], lambda: SC.dma_start(T.aqd[8:128, :], T.aw[0:15, :]))
+    put("s", "aqd", "snd", "x0", "x1", "x2", "x3", "src")
+    put("a", "mp", "aqf", "x4", "x5", "x6", "x7", "bs")
+    for k in range(8):
+        r = slice(16 * k, 16 * k + 16)
+        dma("aw%d" % k, "lpar", ["arr0", "abd0"], lambda r=r: SY.dma_start(T.abd[r, r], T.aw[:]))
+        dma("ab%d" % k, "lpar", [], lambda r=r: SY.dma_start(T.abc[r, 0:1], T.ab[:]))
+        put("s", "aw%d" % k, "ab%d" % k)
+        for q in range(len(cores)):
+            dma("aq%d.%d" % (k, q), "lpar", ["arrq"], lambda r=r, q=q: SY.dma_start(
+                T.aqc[r, q:q + 1], T.aq[:] if q == rank else T.aqin[q, 0:8, :]))
+            put("s", "aq%d.%d" % (k, q))
+    remote("sendq", ["aqd"], lambda: g.remote_dma_fused([RemoteDMATransfer(
+        dst_ids=[dst(q)], dma_engine_mask=small_masks[i], remote_sem=T.sem.arrq,
+        src=T.aqd[:], dst=T.aqin[rank]) for i, q in enumerate(peers)], local_sem=T.sem.sent))
+
+    op("moi", [], lambda: g.iota(T.moi[:], [[1, 3], [3, 8]], 0, 0))
+    op("dif", [], lambda: g.iota(T.dif[:], [[0, 8], [-1, 16]], 0, 1, allow_small_or_imprecise_dtypes=True))
+    op("mpb", ["mp"], lambda: g.partition_broadcast(T.mpb[:], T.mp1[:], 128))
+    op("pi", [], lambda: g.iota(T.pi[:, 0:1], [[1, 1]], 0, 1))
+    op("blk", [], lambda: g.iota(T.blk[:], [[1, 8], [0, 16]], 0, 0, allow_small_or_imprecise_dtypes=True))
+    op("idn", ["ones"], lambda: g.affine_select(T.idn[:], T.ones[:], [[-1, 128]], A.is_equal, 0.0, 0, 1))
+    op("abd0", [], lambda: V.memset(T.abd[:], 0.0))
+    op("ones", [], lambda: V.memset(T.ones[:], 1.0))
+    op("idb", ["idn"], lambda: V.tensor_copy(T.idb[:], T.idn[:]))
+    op("mou", ["moi"], lambda: V.tensor_copy(T.mou[:], T.moi[:]))
+    op("difq", ["dif"], lambda: V.tensor_scalar(T.difq[:], T.dif[:], 1.0 / 16, None, A.mult))
+    op("sndf", ["snd"], lambda: V.tensor_copy(T.sndf[:], T.sndi[:]))
+
+    def perm(s):
+        return T.pmat[:, 128 * s:128 * s + 128]
+    for s in range(S):
+        op("perm%d" % s, ["mpb", "mou", "difq"], lambda s=s: V.tensor_tensor(
+            perm(s), T.mpb[:, 0:24].indirect(T.mou[:, 8 * s:8 * s + 8]), T.difq[:], A.is_equal))
+        op("pbs%d" % s, ["perm%d" % s, "bs"], lambda s=s: PE.matmul(ps[6][:, 256 + s:257 + s], perm(s), T.bsb[:, 0:1], True, True))
+    for i, (name, bank) in enumerate((("src0a", ps[0]), ("src0", ps[4]))):
+        cols = slice(256 * i, 256 * i + 256)
+        op("srcf%d" % i, ["src"], lambda cols=cols: V.tensor_copy(T.srcf[:, cols], T.srci[:, cols]))
+        op("p" + name, ["perm0", "srcf%d" % i], lambda cols=cols, bank=bank: PE.matmul(bank[:, 0:256], perm(0), T.srcf[:, cols], True, True))
+        op(name, ["p" + name], lambda cols=cols, bank=bank: V.tensor_copy(T.src0[:, cols], bank[:, 0:256]))
+    for s in (1, 2):
+        op("psrc%d" % s, ["src%d" % (s - 1)], lambda s=s: PE.matmul(ps[4][:], perm(s), T.srcf[:], True, True))
+        op("src%d" % s, ["psrc%d" % s], lambda s=s: V.tensor_copy(srcu[s][:], ps[4][:]))
+        op("psnd%d" % s, ["perm%d" % s, "sndf"], lambda s=s: PE.matmul(ps[6][:, 128 * (s - 1):128 * s], perm(s), T.sndf[:], True, True))
+    op("psnd0", ["perm0", "sndf"], lambda: PE.matmul(ps[5][:, 0:128], perm(0), T.sndf[:], True, True))
+    op("snd0", ["psnd0"], lambda: V.tensor_copy(T.snd0[:], ps[5][:, 0:128]))
+    psm = ["pbs0", "pbs1", "pbs2", "psnd1", "psnd2"]
+    op("bias4", psm, lambda: V.tensor_scalar(T.bias4[:, 0:3], ps[6][:, 256:259], 4.0, None, A.mult))
+    op("bias1", psm, lambda: V.tensor_copy(T.bias1[:, 0:1], ps[6][:, 258:259]))
+    op("snd12", psm, lambda: V.tensor_copy(T.snd12[:], ps[6][:, 0:256]))
+    op("pg", ["pi"], lambda: V.tensor_scalar(T.pg[:, 0:1], T.pi[:, 0:1], 4, None, A.arith_shift_right))
+    op("pgf", ["pg"], lambda: V.tensor_copy(T.pgf[:, 0:1], T.pg[:, 0:1]))
+    op("aqs", ["aw7"], lambda: V.tensor_scalar(T.aqs[:], T.aqc[:], 2.0 ** -13, None, A.mult))
+    op("m16", ["pgf", "difq"], lambda: V.tensor_scalar(T.m16[:], T.difq[:, 0:16], T.pgf[:, 0:1], None, A.is_equal))
+    for q in range(len(cores)):
+        op("qm%d" % q, ["pgf", "blk", "aqs"], lambda q=q: V.tensor_scalar(
+            T.qm[:, 128 * q:128 * q + 128], T.blk[:], T.pgf[:, 0:1], T.aqs[:, q:q + 1], A.is_equal, A.mult))
+
+    def slots(s, ready):
+        lst, base = (T.snd0, 0) if s == 0 else (T.snd12, 128 * (s - 1))
+        own = T.win0[:, 0:E] if s == 0 else acc[s - 1][:]
+        land = win[s][:, E + CAP * rank:E + CAP * (rank + 1)]
+        h = CAP // 2
+
+        def sg(name, q, out, to, a, b):
+            off = lst[:, base + 32 * to + a // 16:base + 32 * to + b // 16]
+            op("%s%d" % (name, s), ready, lambda: gather(q, out, own, off, relu=s > 0))
+            put(q, "%s%d" % (name, s))
+        sg("sgv", "v", sb[s][:, 0:h], peers[0], 0, h)
+        sg("sga", "a", sb[s][:, h:CAP], peers[0], h, CAP)
+        sg("sgw", "v", sb[s][:, CAP:2 * CAP], peers[1], 0, CAP)
+        sg("sgb", "a", sb[s][:, 2 * CAP:3 * CAP], peers[2], 0, CAP)
+        sg("self", "a", land, rank, 0, CAP)
+
+        def tr(i, mask):
+            return RemoteDMATransfer(dst_ids=[dst(peers[i])], dma_engine_mask=mask, remote_sem=T.sem["arr%d" % s],
+                                     src=sb[s][:, CAP * i:CAP * (i + 1)], dst=land)
+        remote("first%d" % s, ["sgv%d" % s, "sga%d" % s], lambda: g.remote_dma_fused([tr(0, off_mask)], local_sem=T.sem.sent))
+        remote("second%d" % s, ["sgw%d" % s, "sgb%d" % s], lambda: g.remote_dma_fused([tr(1, off_mask), tr(2, on_mask)], local_sem=T.sem.sent))
+        put("g", "first%d" % s, "second%d" % s)
+        if s:
+            for q, a, b in (("v", 0, E // 2), ("a", E // 2, E)):
+                op("own%s%d" % (q, s), ready, lambda q=q, a=a, b=b: finish(q, win[s][:, a:b], acc[s - 1][:, a:b]))
+            put("a", "owna%d" % s)
+
+    att_banks = [0, 1, 2, 3, 5, 6]
+    tanhs = [x for x in ORD["a2"] if x[0] == "t"]
+
+    def step(s):
+        pre = "%d:" % s
+        start = ["arr%d" % s, "self%d" % s, "src%d" % s, "bias4"] + (["ownv%d" % s, "owna%d" % s] if s else ["src0a"])
+        bias = T.bias4[:, s:s + 1]
+        c0 = cc = 0
+        cbanks = [7, 3]
+        done = []
+        for k, (kind, n) in enumerate(CHUNKS[s]):
+            def off(d, c0=c0, n=n):
+                return srcu[s][:, 128 * d + c0 // 16:128 * d + (c0 + n) // 16]
+            rq = "v" if "r%d" % k in ORD["v%d" % s] else "a"
+            a = acc[s][:, c0:c0 + n]
+            h = T.hfin[:, c0 % 512 // 32:(c0 % 512 + n) // 32, c0 // 512, :] if s == S - 1 else None
+            if kind == "C":
+                total = ps[cbanks.pop(0)][:, 0:n]
+                ident = "idb" if s == 0 else "idn"
+                for d in range(4):
+                    gat = cgb[s][:, cc:cc + n]
+                    cc += n
+                    op(pre + "%d.%d" % (k, d), start, lambda gat=gat, d=d, off=off: gather("a", gat, win[s][:], off(d)))
+                    op(pre + "c%d.%d" % (k, d), [pre + "%d.%d" % (k, d), ident], lambda gat=gat, d=d, total=total, ident=ident: PE.matmul(
+                        total, T[ident][:], gat, d == 0, d == 3))
+                last = pre + "c%d.3" % k
+                if s == S - 1:
+                    op(pre + "r%d" % k, [last, "bias1"], lambda h=h, total=total: SC.activation(h, total, F.Relu, bias=T.bias1[:, 0:1], scale=0.25))
+                elif rq == "a":
+                    op(pre + "r%d" % k, [last], lambda a=a, total=total: SC.activation(a, total, F.Identity, bias=bias))
+                else:
+                    op(pre + "r%d" % k, [last], lambda a=a, total=total: V.tensor_scalar(a, total, bias, None, A.add))
+                done.append(pre + "r%d" % k)
+            else:
+                op(pre + "%d.0" % k, start, lambda a=a, off=off, kind=kind: gather("v" if kind == "D" else "a", a, win[s][:], off(0), bias))
+                for d in (1, 2, 3):
+                    op(pre + "%d.%d" % (k, d), start + [pre + "%d.%d" % (k, d - 1)], lambda a=a, d=d, off=off: V.tensor_tensor(
+                        a, win[s][:].indirect(off(d)), a, A.add))
+                done.append(pre + "%d.3" % k)
+                if s == S - 1:
+                    op(pre + "r%d" % k, [pre + "%d.3" % k], lambda h=h, a=a, rq=rq: finish(rq, h, a))
+            if s == S - 1:
+                bank = ps[att_banks[k]][:, 0:n]
+                col = 6 if tanhs[-1] == "t%d" % k else tanhs.index("t%d" % k)
+                op(pre + "m%d" % k, [pre + "r%d" % k, "aw7"], lambda bank=bank, h=h: PE.matmul(bank, T.abd[:], h, True, True))
+                op(pre + "t%d" % k, [pre + "m%d" % k, "aw7"], lambda bank=bank, col=col, c0=c0, n=n: SC.activation(
+                    T.tnh[:, c0:c0 + n], bank, F.Tanh, bias=T.abc[:, 0:1], accum_out=T.tsum[:, col:col + 1]))
+            c0 += n
+        for q in "vap":
+            put(q, *[pre + x for x in ORD["%s%d" % (q, s)]])
+        return done
+
+    put("g", "moi", "dif", "idn", "mpb", "sendq")
+    put("v", "ones", "mou", "difq", "abd0", "idb", "sndf", "perm0", "perm1", "snd0", "perm2")
+    put("p", "psnd0", *psm, "psrc0a", "psrc0")
+    slots(0, ["x0", "snd0"])
+    put("g", "pi", "blk")
+    put("v", "srcf0", "srcf1", "bias4", "bias1", "src0a", "src0", "snd12")
+    done = step(0)
+    put("p", "psrc1")
+    slots(1, done + ["snd12"])
+    put("v", "pg", "ownv1", "src1", "pgf", "aqs", "m16")
+    done = step(1)
+    put("p", "psrc2")
+    slots(2, done)
+    put("v", "ownv2", "src2", "qm0", "qm1", "qm2", "qm3")
+    step(2)
+
+    tl = "2:" + tanhs[-1]
+    op("tpart", ["2:" + x for x in tanhs[:-1]], lambda: V.tensor_reduce(T.tsum[:, 7:8], T.tsum[:, 0:len(tanhs) - 1], AxisListType.X, A.add))
+    remote("sends", ["tpart", tl], lambda: g.remote_dma_fused([RemoteDMATransfer(
+        dst_ids=[dst(q)], dma_engine_mask=small_masks[i], remote_sem=T.sem["arrf" if q in far else "arrn"],
+        src=T.tsum[:, 6:8], dst=T.sin[:, 2 * rank:2 * rank + 2]) for i, q in enumerate(peers)], local_sem=T.sem.sent))
+
+    def score(q, out, start, stop):
+        return PE.matmul(out, T.qm[:, 128 * q:128 * q + 128], T.tsum[:, 6:8] if q == rank else T.sin[:, 2 * q:2 * q + 2], start, stop)
+    op("sco", ["tpart", tl, "qm3", "src2"], lambda: score(rank, ps[4][:, 0:2], True, True))
+    op("scn", ["arrn"], lambda: score(near[0], ps[7][:, 0:2], True, False))
+    op("scf0", ["arrf"], lambda: score(far[0], ps[7][:, 0:2], False, False))
+    op("scf1", ["arrf"], lambda: score(far[1], ps[7][:, 0:2], False, True))
+    op("exo", ["sco"], lambda: SC.activation(T.exo[:, 0:2], ps[4][:, 0:2], F.Exp))
+    op("mx", ["exo", "m16"], lambda: V.tensor_scalar(T.mx[:], T.m16[:], T.exo[:, 0:1], T.exo[:, 1:2], A.mult, A.mult))
+    op("exr", ["scf1"], lambda: SC.activation(T.exr[:, 0:2], ps[7][:, 0:2], F.Exp))
+    op("wm", ["mx", "exr"], lambda: V.tensor_scalar(T.wm[:], T.mx[:], T.exr[:, 0:1], T.exr[:, 1:2], A.mult, A.mult))
+    dma("ow", "ow", ["wm"], lambda: SY.dma_start(T.w[:], T.wm[0:128:16, 0:1]))
+    put("p", "sco", "scn", "scf0", "scf1")
+    put("v", "tpart", "mx", "wm")
+    put("g", "sends")
+    put("a", "exo", "exr")
+    put("s", "ow")
+
+    for half in range(2):
+        names = []
+        for b in range(4 * half, 4 * half + 4):
+            for u in range(2):
+                names.append("y%d.%d" % (b, u))
+                op(names[-1], ["wm"], lambda half=half, b=b, u=u: PE.matmul(
+                    ps[half][:, 32 * (b % 4) + u:32 * (b % 4) + 32:2], T.hfin[:, 8 * u + b], T.wm[:], True, True))
+        op("yo%d" % half, names, lambda half=half: V.transpose(T.yo[:, 128 * half:128 * half + 128], ps[half][:, 0:128]))
+        put("p", *names)
+        put("v", "yo%d" % half)
+    for a in range(4):
+        dma("yd%d" % a, "oy", ["yo0", "yo1"], lambda a=a: (SY if a % 2 else SC).dma_start(
+            T.y[:, 512 * a:512 * a + 512], T.yo[32 * a:32 * a + 32, :]))
+        put("s" if a % 2 else "a", "yd%d" % a)
+
+    total = dict(dmas)
+    for q, names in order.items():
+        n = 0
+        for name in names:
+            kind = ops[name][2]
+            if kind is None:
+                n += 1
+                tok[name] = ("c" + q, n)
+            elif kind != "remote":
+                tok[name] = (kind, dmas[kind])
+        if q != "s":
+            total["c" + q] = n
+    seen = {}
+    for q, names in order.items():
+        for name in names:
+            deps, fn, kind = ops[name]
+            want = {}
+            for dname in deps:
+                sem, val = tok[dname]
+                want[sem] = max(want.get(sem, 0), val)
+            for sem, val in want.items():
+                if seen.get((q, sem), 0) < val:
+                    eng[q].wait_ge(T.sem[sem], val)
+                    seen[(q, sem)] = val
+            ins = fn()
+            if kind is None:
+                ins.then_inc(T.sem["c" + q], 1)
+            elif kind != "remote":
+                ins.then_inc(T.sem[kind], 16)
+    total["sent"] = S * n_slots + 2 * n_small
+    for sem, val in total.items():
+        if max(seen.get((q, sem), 0) for q in eng) < val:
+            g.wait_ge(T.sem[sem], val)

@@ -2,27 +2,27 @@ from concourse.bass import DstId, RemoteDMATransfer
 from concourse.mybir import AluOpType, AxisListType, ActivationFunctionType
 
 E, CAP, P, S = 2048, 512, 4096, 3
-F32, BF, I32, U16 = "float32", "bfloat16", "int32", "uint16"
+F32, BF, F16, I32, U16 = "float32", "bfloat16", "float16", "int32", "uint16"
 
 SCRATCH = {
     "win0": ("sbuf", [128, P], BF), "win1": ("sbuf", [128, P], F32), "win2": ("sbuf", [128, P], F32),
     "hfin": ("sbuf", [128, 16, 4, 32], F32),
     "sb0": ("sbuf", [128, 3 * CAP], BF), "sb1": ("sbuf", [128, 3 * CAP], F32), "sb2": ("sbuf", [128, 3 * CAP], F32),
-    "acc0": ("sbuf", [128, E], F32), "acc1": ("sbuf", [128, E], F32), "acc2": ("sbuf", [128, E], F32),
+    "acc2": ("sbuf", [128, E], F32),
     "cg0": ("sbuf", [128, 4 * 768], BF), "cg1": ("sbuf", [128, 4 * 768], F32), "cg2": ("sbuf", [128, 4 * 768], F32),
-    "srci": ("sbuf", [128, 512], I32), "sndi": ("sbuf", [128, 128], I32),
-    "srcf": ("sbuf", [128, 512], F32), "sndf": ("sbuf", [128, 128], F32),
+    "srci": ("sbuf", [128, 4, 128], I32), "sndi": ("sbuf", [128, 128], I32),
+    "srcf": ("sbuf", [128, 4, 128], F16), "sndf": ("sbuf", [128, 128], F16),
     "src0": ("sbuf", [128, 512], U16), "src1": ("sbuf", [128, 512], U16), "src2": ("sbuf", [128, 512], U16),
     "snd0": ("sbuf", [128, 128], U16), "snd12": ("sbuf", [128, 256], U16),
-    "bsb": ("sbuf", [128, 4], F32), "bias4": ("sbuf", [128, 4], F32), "bias1": ("sbuf", [128, 4], F32),
+    "bsb": ("sbuf", [128, 4], F32), "bias": ("sbuf", [128, 4], F32), "bsc": ("sbuf", [128, 4], F32),
     "mp1": ("sbuf", [1, 24], I32), "mpb": ("sbuf", [128, 24], I32),
     "moi": ("sbuf", [128, 24], I32), "mou": ("sbuf", [128, 24], U16),
-    "dif": ("sbuf", [128, 128], F32), "difq": ("sbuf", [128, 128], F32), "pmat": ("sbuf", [128, 384], F32),
+    "dif": ("sbuf", [128, 128], F32), "difq": ("sbuf", [128, 128], F32),
+    "pmat": ("sbuf", [128, 384], BF), "pm32": ("sbuf", [128, 384], F32),
     "ones": ("sbuf", [128, 128], F32), "idn": ("sbuf", [128, 128], F32), "idb": ("sbuf", [128, 128], BF),
     "pi": ("sbuf", [128, 4], I32), "pg": ("sbuf", [128, 4], I32), "pgf": ("sbuf", [128, 4], F32),
-    "blk": ("sbuf", [128, 128], F32), "qm": ("sbuf", [128, 512], F32), "m16": ("sbuf", [128, 16], F32),
+    "blk": ("sbuf", [128, 24], F32), "qm": ("sbuf", [128, 512], F32), "m16": ("sbuf", [128, 16], F32),
     "abd": ("sbuf", [128, 128], F32), "abc": ("sbuf", [128, 4], F32), "aqc": ("sbuf", [128, 4], F32),
-    "aqs": ("sbuf", [128, 4], F32),
     "aqd": ("dram", [128, 2], F32), "aqin": ("dram", [4, 128, 2], F32),
     "tnh": ("sbuf", [128, E], F32), "tsum": ("sbuf", [128, 8], F32),
     "sin": ("sbuf", [128, 8], F32), "exo": ("sbuf", [128, 4], F32), "exr": ("sbuf", [128, 4], F32),
@@ -33,54 +33,85 @@ for _b in range(8):
     SCRATCH["ps%d" % _b] = ("psum", [128, 512], F32)
 
 SEMAPHORES = ["cv", "ca", "cp", "cg", "lx", "lsnd", "lsrc", "lmp", "lbs", "lpar", "laq", "sent",
-              "arr0", "arr1", "arr2", "arrq", "arrn", "arrf", "ow", "oy"]
+              "arr0", "arr1", "arr2", "relq", "rel0_0", "rel0_1", "rel1_0", "rel1_1", "rel2_0", "rel2_1", "arrq", "arrn", "arrf0", "arrf1", "ow", "oy"]
 
 CHUNKS = [
-    [("D", 256), ("A", 512), ("A", 320), ("A", 256), ("C", 512), ("C", 192)],
-    [("D", 256), ("A", 512), ("A", 384), ("A", 256), ("C", 512), ("C", 128)],
-    [("D", 256), ("A", 256), ("A", 512), ("A", 512), ("A", 128), ("C", 384)],
+    [("D", 288), ("A", 128), ("A", 928), ("C", 416), ("C", 288)],
+    [("D", 256), ("A", 128), ("A", 480), ("A", 448), ("H", 480), ("H", 256)],
+    [("D", 384), ("A", 128), ("A", 224), ("A", 288), ("A", 512), ("A", 96), ("C", 416)],
 ]
 ORD = {
-    "v0": "0.0 0.1 1.1 0.2 3.1 1.2 2.1 0.3 2.2 3.2 1.3 2.3 3.3".split(),
-    "a0": "1.0 3.0 4.0 2.0 4.1 4.2 4.3 5.0 5.1 5.2 5.3 r4 r5".split(),
-    "p0": "c4.0 c4.1 c4.2 c4.3 c5.0 c5.1 c5.2 c5.3".split(),
-    "v1": "0.0 0.1 0.2 3.1 0.3 3.2 2.1 3.3 2.2 1.1 2.3 1.2 1.3".split(),
-    "a1": "4.0 3.0 4.1 2.0 4.2 1.0 5.0 5.1 4.3 5.2 5.3 r4 r5".split(),
-    "p1": "c4.0 c4.1 c4.2 c5.0 c5.1 c4.3 c5.2 c5.3".split(),
-    "v2": "0.0 0.1 2.1 0.2 2.2 0.3 3.1 2.3 3.2 4.1 3.3 1.1 r3 1.2 4.2 1.3 r1 4.3 r4".split(),
-    "a2": "2.0 5.0 5.1 3.0 5.2 5.3 r0 4.0 1.0 r2 r5 t0 t2 t5 t3 t1 t4".split(),
-    "p2": "c5.0 c5.1 c5.2 c5.3 m0 m2 m5 m3 m1 m4".split(),
+    "v0": "0.0 1.1 0.1 1.2 0.2 2.1 0.3 2.2 1.3 2.3".split(),
+    "a0": "1.0 2.0 3.0123 4.012 4.3 r3 r4".split(),
+    "p0": "c3.0 c3.1 c3.2 c3.3 c4.0 c4.1 c4.2 c4.3".split(),
+    "v1": "0.0 1.1 0.1 1.2 0.2 1.3 2.1 0.3 2.2 3.1 2.3 3.2 r4 3.3 r5".split(),
+    "a1": "1.0 4.1 2.0 5.1 4.2 3.0 4.3 5.2 4.0 5.3 5.0 r0 r1 qm0".split(),
+    "p1": "c4.1 c5.1 c4.2 c4.3 c5.2 c5.3".split(),
+    "v2": "0.0 0.1 2.1 0.2 2.2 0.3 4.1 2.3 4.2 3.1 4.3 3.2 1.1 3.3 5.1 1.2 5.2 1.3 5.3 r1 r5".split(),
+    "a2": "6.0 2.0 6.1 6.2 4.0 6.3 3.0 r0 r2 5.0 1.0 r6 r4 t2 t0 r3 t6 t4 t3 t1 t5".split(),
+    "p2": "c6.0 c6.1 c6.2 c6.3 m0 m2 m6 m4 m3 m1 m5".split(),
 }
+ATT_BANKS = [1, 5, 0, 4, 3, 6, 2]
+SLOTS = [("v", 0, 0, 128), ("a", 1, 256, 384), ("v", 0, 128, 256), ("a", 1, 384, 512), ("v", 0, 256, 512), ("a", 2, 0, 256),
+         ("v", 1, 0, 256), ("a", 2, 256, 512), ("v", None, 0, 192), ("a", None, 192, 512)]
+CALLS = [[(0, 0, 128), ("h", 256, 384)], [(0, 128, 256), ("h", 384, 512)], [(0, 256, 512), (2, 0, 256)], [(1, 0, 256), (2, 256, 512)]]
+SLOTS0 = [("v", 0, 0, 256), ("a", 0, 256, 512), ("v", 1, 0, 512), ("a", 2, 0, 512), ("a", None, 0, 512)]
+CALLS0 = [[(0, 0, 512)], [(1, 0, 512), (2, 0, 512)]]
+FINISH_V = [576, 672]
+START = {
+    "g": "blk0 moi dif mpb sendq pi idn".split(),
+    "v": "ones bsc abd0 mou difq sndf perm0 perm1 snd0 perm2".split(),
+    "a": "blk1 blk".split(),
+    "p": "psnd0 psn psrc0 pb".split(),
+}
+FILL = ["srcf snd12 src0 bias".split(), ["src1"], ["src2"]]
+PARTS = [(0, 4), (4, 8)]
 
 
 def rank_program(g, core, T, topo):
+    cores = list(T.cores)
+
+    def places(rank):
+        me = cores[rank]
+        near = [q for q in range(len(cores)) if q != rank and topo.chip(cores[q]) == topo.chip(me)]
+        far = [q for q in range(len(cores)) if topo.chip(cores[q]) != topo.chip(me)]
+        far.sort(key=lambda q: topo.die(cores[q]) == topo.die(me))
+        helper = [c for c in topo.cores_of(me) if c not in cores and topo.die(c) == topo.die(me) and topo.may_write(c, cores[far[-1]])]
+        return far, near, helper[0]
+
+    def write(parts):
+        return g.remote_dma_fused([RemoteDMATransfer(
+            dst_ids=[DstId(rid=topo.addr(c)[0], pnc=topo.addr(c)[1])], dma_engine_mask=sum(1 << e for e in engines),
+            remote_sem=T.sem[sem], src=src, dst=land) for c, engines, sem, src, land in parts], local_sem=T.sem.sent)
+
+    relayed = [[(a, b) for call in (CALLS if s else CALLS0) for blk, a, b in call if blk == "h"] for s in range(S)]
     rank = T.rank_of(core)
     if rank is None:
+        for r in range(len(cores)):
+            far, near, helper = places(r)
+            if helper == core:
+                to = cores[far[-1]]
+                out = topo.engines(core, to)
+                n_in = len([e for e in topo.engines(cores[r], core) if e not in out])
+                g.wait_ge(T.sem.relq, n_in // 2)
+                write([(to, out, "arrq", T.aqd[:], T.aqin[r])])
+                for s in range(S):
+                    for i, (a, b) in enumerate(relayed[s]):
+                        g.wait_ge(T.sem["rel%d_%d" % (s, i)], n_in)
+                        write([(to, out, "arr%d" % s, T["sb%d" % s][:, a:b], T["win%d" % s][:, E + CAP * r + a:E + CAP * r + b])])
+                g.wait_ge(T.sem.sent, len(out) * (1 + sum(len(pieces) for pieces in relayed)))
         return
     A, F = AluOpType, ActivationFunctionType
     V, SC, PE, SY = g.vector, g.scalar, g.tensor, g.sync
     eng = {"v": V, "a": SC, "p": PE, "g": g, "s": SY}
-    cores = list(T.cores)
-    near = [q for q in range(len(cores)) if q != rank and topo.chip(cores[q]) == topo.chip(core)]
-    far = [q for q in range(len(cores)) if topo.chip(cores[q]) != topo.chip(core)]
-    far.sort(key=lambda q: topo.die(cores[q]) == topo.die(core))
+    far, near, helper = places(rank)
     peers = far + near
     off_eng = topo.engines(core, cores[far[0]])
     on_eng = [e for e in topo.engines(core, cores[near[0]]) if e not in off_eng]
-    off_mask, on_mask = sum(1 << e for e in off_eng), sum(1 << e for e in on_eng)
-    share = len(off_eng) // len(far)
-    small_masks = [sum(1 << e for e in off_eng[i * share:(i + 1) * share]) for i in range(len(far))] + [on_mask]
-    n_slots = len(far) * len(off_eng) + len(on_eng)
-    n_small = share * len(far) + len(on_eng)
-
-    def dst(q):
-        rid, pid, _ = topo.addr(cores[q])
-        return DstId(rid=rid, pnc=pid)
+    block_eng = [off_eng] * len(far) + [on_eng]
 
     ops, order = {}, {q: [] for q in eng}
-    tok = {"arr0": ("arr0", n_slots), "arr1": ("arr1", n_slots), "arr2": ("arr2", n_slots), "arrq": ("arrq", n_small),
-           "arrn": ("arrn", len(on_eng)), "arrf": ("arrf", share * len(far))}
-    dmas = {}
+    tok, dmas, many = {}, {}, {}
 
     def op(name, deps, fn):
         ops[name] = (deps, fn, None)
@@ -89,11 +120,20 @@ def rank_program(g, core, T, topo):
         ops[name] = (deps, fn, sem)
         dmas[sem] = dmas.get(sem, 0) + 16
 
-    def remote(name, deps, fn):
-        ops[name] = (deps, fn, "remote")
+    def remote(name, deps, parts):
+        ops[name] = (deps, lambda: write([part[:5] for part in parts]), "remote")
+        for part in parts:
+            for s, n in (("sent", len(part[1])), (part[5], len(off_eng)) if part[0] == helper else (part[2], len(part[1]))):
+                tok[s] = (s, tok.get(s, (s, 0))[1] + n)
 
     def put(q, *names):
-        order[q].extend(names)
+        for name in names:
+            order[q].extend(many.get(name, [name]))
+
+    def matmuls(name, deps, calls):
+        many[name] = ["%s#%d" % (name, i) for i in range(len(calls) - 1)] + [name]
+        for nm, c in zip(many[name], calls):
+            op(nm, deps, lambda c=c: PE.matmul(*c))
 
     def gather(q, out, win, off, bias=None, relu=False):
         src = win.indirect(off)
@@ -107,17 +147,18 @@ def rank_program(g, core, T, topo):
             return V.tensor_copy(out, src)
         return V.tensor_scalar(out, src, bias, None, A.add)
 
-    def finish(q, out, total):
+    def finish(q, out, total, scale=1.0):
         if q == "a":
-            return SC.activation(out, total, F.Relu, scale=0.25)
-        return V.tensor_scalar(out, total, 0.25, 0.0, A.mult, A.max)
+            return SC.activation(out, total, F.Relu, scale=scale)
+        return V.tensor_scalar(out, total, scale, 0.0, A.mult, A.max)
 
     ps = [T["ps%d" % b] for b in range(8)]
     win = [T.win0, T.win1, T.win2]
     sb = [T.sb0, T.sb1, T.sb2]
     srcu = [T.src0, T.src1, T.src2]
-    acc = [T.acc0, T.acc1, T.acc2]
+    acc = [T.win1, T.win2, T.acc2]
     cgb = [T.cg0, T.cg1, T.cg2]
+    last_scale = 0.25 ** S
 
     for k in range(8):
         dma("x%d" % k, "lx", [], lambda k=k, q=(SY if k < 4 else SC): q.dma_start(T.win0[16 * k:16 * k + 16, 0:E], T.x[:]))
@@ -138,111 +179,136 @@ def rank_program(g, core, T, topo):
             dma("aq%d.%d" % (k, q), "lpar", ["arrq"], lambda r=r, q=q: SY.dma_start(
                 T.aqc[r, q:q + 1], T.aq[:] if q == rank else T.aqin[q, 0:8, :]))
             put("s", "aq%d.%d" % (k, q))
-    remote("sendq", ["aqd"], lambda: g.remote_dma_fused([RemoteDMATransfer(
-        dst_ids=[dst(q)], dma_engine_mask=small_masks[i], remote_sem=T.sem.arrq,
-        src=T.aqd[:], dst=T.aqin[rank]) for i, q in enumerate(peers)], local_sem=T.sem.sent))
+    half_on = len(on_eng) // 2
+    remote("sendq", ["aqd"], [(cores[far[0]], off_eng, "arrq", T.aqd[:], T.aqin[rank]),
+                              (cores[near[0]], on_eng[:half_on], "arrq", T.aqd[:], T.aqin[rank]),
+                              (helper, on_eng[half_on:], "relq", T.aqd[:], T.aqd[:], "arrq")])
 
     op("moi", [], lambda: g.iota(T.moi[:], [[1, 3], [3, 8]], 0, 0))
     op("dif", [], lambda: g.iota(T.dif[:], [[0, 8], [-1, 16]], 0, 1, allow_small_or_imprecise_dtypes=True))
     op("mpb", ["mp"], lambda: g.partition_broadcast(T.mpb[:], T.mp1[:], 128))
     op("pi", [], lambda: g.iota(T.pi[:, 0:1], [[1, 1]], 0, 1))
-    op("blk", [], lambda: g.iota(T.blk[:], [[1, 8], [0, 16]], 0, 0, allow_small_or_imprecise_dtypes=True))
     op("idn", ["ones"], lambda: g.affine_select(T.idn[:], T.ones[:], [[-1, 128]], A.is_equal, 0.0, 0, 1))
+    op("blk0", [], lambda: g.iota(T.blk[:], [[-32, 8], [0, S]], -15, 2, allow_small_or_imprecise_dtypes=True))
+    op("blk1", ["blk0"], lambda: SC.activation(T.blk[:], T.blk[:], F.Square))
+    op("blk", ["blk1", "bsc"], lambda: SC.activation(T.blk[:], T.blk[:], F.Tanh, bias=T.bsc[:, 3:4], scale=-1.0))
     op("abd0", [], lambda: V.memset(T.abd[:], 0.0))
     op("ones", [], lambda: V.memset(T.ones[:], 1.0))
-    op("idb", ["idn"], lambda: V.tensor_copy(T.idb[:], T.idn[:]))
+    many["bsc"] = ["bsc0", "bsc1", "bsc2", "bsc"]
+    for i, (name, val) in enumerate(zip(many["bsc"], (4.0, 16.0, 64.0, 257.0))):
+        op(name, [], lambda i=i, val=val: V.memset(T.bsc[:, i:i + 1], val))
+    op("idb", ["idn"], lambda: SC.activation(T.idb[:], T.idn[:], F.Copy))
     op("mou", ["moi"], lambda: V.tensor_copy(T.mou[:], T.moi[:]))
     op("difq", ["dif"], lambda: V.tensor_scalar(T.difq[:], T.dif[:], 1.0 / 16, None, A.mult))
     op("sndf", ["snd"], lambda: V.tensor_copy(T.sndf[:], T.sndi[:]))
+    op("srcf", ["src"], lambda: V.tensor_scalar(T.srcf[:], T.srci[:], -float(E), None, A.add))
 
-    def perm(s):
-        return T.pmat[:, 128 * s:128 * s + 128]
+    def perm(s, m=T.pmat):
+        return m[:, 128 * s:128 * s + 128]
     for s in range(S):
         op("perm%d" % s, ["mpb", "mou", "difq"], lambda s=s: V.tensor_tensor(
             perm(s), T.mpb[:, 0:24].indirect(T.mou[:, 8 * s:8 * s + 8]), T.difq[:], A.is_equal))
-        op("pbs%d" % s, ["perm%d" % s, "bs"], lambda s=s: PE.matmul(ps[6][:, 256 + s:257 + s], perm(s), T.bsb[:, 0:1], True, True))
-    for i, (name, bank) in enumerate((("src0a", ps[0]), ("src0", ps[4]))):
-        cols = slice(256 * i, 256 * i + 256)
-        op("srcf%d" % i, ["src"], lambda cols=cols: V.tensor_copy(T.srcf[:, cols], T.srci[:, cols]))
-        op("p" + name, ["perm0", "srcf%d" % i], lambda cols=cols, bank=bank: PE.matmul(bank[:, 0:256], perm(0), T.srcf[:, cols], True, True))
-        op(name, ["p" + name], lambda cols=cols, bank=bank: V.tensor_copy(T.src0[:, cols], bank[:, 0:256]))
-    for s in (1, 2):
-        op("psrc%d" % s, ["src%d" % (s - 1)], lambda s=s: PE.matmul(ps[4][:], perm(s), T.srcf[:], True, True))
-        op("src%d" % s, ["psrc%d" % s], lambda s=s: V.tensor_copy(srcu[s][:], ps[4][:]))
-        op("psnd%d" % s, ["perm%d" % s, "sndf"], lambda s=s: PE.matmul(ps[6][:, 128 * (s - 1):128 * s], perm(s), T.sndf[:], True, True))
+    op("pm32", ["perm0", "perm1", "perm2"], lambda: SC.activation(T.pm32[:], T.pmat[:], F.Copy))
+    for s in range(S):
+        calls, c0 = [], 0
+        for kind, n in CHUNKS[s]:
+            calls.append((ps[4][:, c0 // 4:(c0 + n) // 4], perm(s), T.srcf[:, :, c0 // 16:(c0 + n) // 16], True, True))
+            c0 += n
+        matmuls("psrc%d" % s, ["perm%d" % s, "srcf"] + (["src%d" % (s - 1)] if s else []), calls)
+        op("src%d" % s, ["psrc%d" % s], lambda s=s: V.tensor_scalar(srcu[s][:], ps[4][:], float(E), None, A.add))
     op("psnd0", ["perm0", "sndf"], lambda: PE.matmul(ps[5][:, 0:128], perm(0), T.sndf[:], True, True))
     op("snd0", ["psnd0"], lambda: V.tensor_copy(T.snd0[:], ps[5][:, 0:128]))
-    psm = ["pbs0", "pbs1", "pbs2", "psnd1", "psnd2"]
-    op("bias4", psm, lambda: V.tensor_scalar(T.bias4[:, 0:3], ps[6][:, 256:259], 4.0, None, A.mult))
-    op("bias1", psm, lambda: V.tensor_copy(T.bias1[:, 0:1], ps[6][:, 258:259]))
-    op("snd12", psm, lambda: V.tensor_copy(T.snd12[:], ps[6][:, 0:256]))
+    matmuls("pb", ["pm32", "bs", "snd0"], [(ps[5][:, 256 + s:257 + s], perm(s, T.pm32), T.bsb[:, 0:1], True, True) for s in range(S)])
+    matmuls("psn", ["perm1", "perm2", "sndf"], [(ps[6][:, 128 * (s - 1):128 * s], perm(s), T.sndf[:], True, True) for s in (1, 2)])
+    op("bias1", ["bias"], lambda: SC.activation(T.bias[:, 3:4], ps[5][:, 258:259], F.Copy))
+    op("bias", ["pb", "bsc"], lambda: V.tensor_tensor(T.bias[:, 0:3], ps[5][:, 256:259], T.bsc[:, 0:3], A.mult))
+    op("snd12", ["psn"], lambda: V.tensor_copy(T.snd12[:], ps[6][:, 0:256]))
     op("pg", ["pi"], lambda: V.tensor_scalar(T.pg[:, 0:1], T.pi[:, 0:1], 4, None, A.arith_shift_right))
     op("pgf", ["pg"], lambda: V.tensor_copy(T.pgf[:, 0:1], T.pg[:, 0:1]))
-    op("aqs", ["aw7"], lambda: V.tensor_scalar(T.aqs[:], T.aqc[:], 2.0 ** -13, None, A.mult))
     op("m16", ["pgf", "difq"], lambda: V.tensor_scalar(T.m16[:], T.difq[:, 0:16], T.pgf[:, 0:1], None, A.is_equal))
-    for q in range(len(cores)):
-        op("qm%d" % q, ["pgf", "blk", "aqs"], lambda q=q: V.tensor_scalar(
-            T.qm[:, 128 * q:128 * q + 128], T.blk[:], T.pgf[:, 0:1], T.aqs[:, q:q + 1], A.is_equal, A.mult))
+    for i, q in enumerate([rank] + near + far):
+        out, aq = T.qm[:, 128 * q:128 * q + 128], T.aqc[:, q:q + 1]
+        wide = T.blk[:].indirect(T.mou[:, 0:8])
+        if "qm%d" % i in ORD["a1"]:
+            op("qm%d" % i, ["blk", "mou", "aw7"], lambda out=out, aq=aq, wide=wide: SC.activation(out, wide, F.Identity, bias=aq, scale=aq))
+        else:
+            op("qm%d" % i, ["blk", "mou", "aw7"], lambda out=out, aq=aq, wide=wide: V.tensor_scalar(out, wide, 1.0, aq, A.add, A.mult))
 
-    def slots(s, ready):
+    def slots(s, ready, cut):
         lst, base = (T.snd0, 0) if s == 0 else (T.snd12, 128 * (s - 1))
-        own = T.win0[:, 0:E] if s == 0 else acc[s - 1][:]
-        land = win[s][:, E + CAP * rank:E + CAP * (rank + 1)]
-        h = CAP // 2
-
-        def sg(name, q, out, to, a, b):
+        at = E + CAP * rank
+        names = []
+        for i, (q, blk, a, b) in enumerate(SLOTS if s else SLOTS0):
+            to = rank if blk is None else peers[blk]
+            out = win[s][:, at + a:at + b] if blk is None else sb[s][:, CAP * blk + a:CAP * blk + b]
             off = lst[:, base + 32 * to + a // 16:base + 32 * to + b // 16]
-            op("%s%d" % (name, s), ready, lambda: gather(q, out, own, off, relu=s > 0))
-            put(q, "%s%d" % (name, s))
-        sg("sgv", "v", sb[s][:, 0:h], peers[0], 0, h)
-        sg("sga", "a", sb[s][:, h:CAP], peers[0], h, CAP)
-        sg("sgw", "v", sb[s][:, CAP:2 * CAP], peers[1], 0, CAP)
-        sg("sgb", "a", sb[s][:, 2 * CAP:3 * CAP], peers[2], 0, CAP)
-        sg("self", "a", land, rank, 0, CAP)
-
-        def tr(i, mask):
-            return RemoteDMATransfer(dst_ids=[dst(peers[i])], dma_engine_mask=mask, remote_sem=T.sem["arr%d" % s],
-                                     src=sb[s][:, CAP * i:CAP * (i + 1)], dst=land)
-        remote("first%d" % s, ["sgv%d" % s, "sga%d" % s], lambda: g.remote_dma_fused([tr(0, off_mask)], local_sem=T.sem.sent))
-        remote("second%d" % s, ["sgw%d" % s, "sgb%d" % s], lambda: g.remote_dma_fused([tr(1, off_mask), tr(2, on_mask)], local_sem=T.sem.sent))
-        put("g", "first%d" % s, "second%d" % s)
+            names.append("g%d.%d" % (s, i))
+            op(names[-1], ready, lambda q=q, out=out, off=off: gather(q, out, win[s][:, 0:E], off, relu=s > 0))
+            put(q, names[-1])
+        for i, call in enumerate(CALLS if s else CALLS0):
+            deps, parts = [], []
+            for via, a, b in call:
+                blk = len(far) - 1 if via == "h" else via
+                deps += [names[k] for k, (q, blk2, a2, b2) in enumerate(SLOTS if s else SLOTS0) if blk == blk2 and a < b2 and a2 < b]
+                src = sb[s][:, CAP * blk + a:CAP * blk + b]
+                if via == "h":
+                    parts.append((helper, on_eng, "rel%d_%d" % (s, relayed[s].index((a, b))), src, sb[s][:, a:b], "arr%d" % s))
+                else:
+                    engines = block_eng[blk]
+                    alike = [piece for piece in call if piece[0] != "h" and block_eng[piece[0]] == engines]
+                    n = len(engines) // len(alike)
+                    k = alike.index((via, a, b))
+                    parts.append((cores[peers[blk]], engines[k * n:(k + 1) * n], "arr%d" % s, src, win[s][:, at + a:at + b]))
+            remote("send%d.%d" % (s, i), deps, parts)
+            put("g", "send%d.%d" % (s, i))
+        put("v", *FILL[s][:1])
         if s:
-            for q, a, b in (("v", 0, E // 2), ("a", E // 2, E)):
-                op("own%s%d" % (q, s), ready, lambda q=q, a=a, b=b: finish(q, win[s][:, a:b], acc[s - 1][:, a:b]))
-            put("a", "owna%d" % s)
+            mid = cut[0] + FINISH_V[s - 1]
+            for q, a, b in (("v", cut[0], mid), ("a", mid, cut[1])):
+                op("own%s%d" % (q, s), names, lambda q=q, a=a, b=b: finish(q, win[s][:, a:b], win[s][:, a:b]))
+                put(q, "own%s%d" % (q, s))
+            names = names + ["ownv%d" % s, "owna%d" % s]
+        put("v", *FILL[s][1:])
+        return names + ["arr%d" % s, "src%d" % s, "bias"]
 
-    att_banks = [0, 1, 2, 3, 5, 6]
     tanhs = [x for x in ORD["a2"] if x[0] == "t"]
 
-    def step(s):
+    def step(s, start):
         pre = "%d:" % s
-        start = ["arr%d" % s, "self%d" % s, "src%d" % s, "bias4"] + (["ownv%d" % s, "owna%d" % s] if s else ["src0a"])
-        bias = T.bias4[:, s:s + 1]
-        c0 = cc = 0
+        bias = T.bias[:, s:s + 1]
+        c0 = cc = cut = 0
         cbanks = [7, 3]
         done = []
         for k, (kind, n) in enumerate(CHUNKS[s]):
-            def off(d, c0=c0, n=n):
-                return srcu[s][:, 128 * d + c0 // 16:128 * d + (c0 + n) // 16]
+            def off(d, m=1, c0=c0, n=n):
+                at = c0 // 4 + d * n // 16
+                return srcu[s][:, at:at + m * n // 16]
             rq = "v" if "r%d" % k in ORD["v%d" % s] else "a"
             a = acc[s][:, c0:c0 + n]
             h = T.hfin[:, c0 % 512 // 32:(c0 % 512 + n) // 32, c0 // 512, :] if s == S - 1 else None
-            if kind == "C":
+            if kind in "CH":
                 total = ps[cbanks.pop(0)][:, 0:n]
                 ident = "idb" if s == 0 else "idn"
-                for d in range(4):
-                    gat = cgb[s][:, cc:cc + n]
-                    cc += n
-                    op(pre + "%d.%d" % (k, d), start, lambda gat=gat, d=d, off=off: gather("a", gat, win[s][:], off(d)))
-                    op(pre + "c%d.%d" % (k, d), [pre + "%d.%d" % (k, d), ident], lambda gat=gat, d=d, total=total, ident=ident: PE.matmul(
-                        total, T[ident][:], gat, d == 0, d == 3))
-                last = pre + "c%d.3" % k
-                if s == S - 1:
-                    op(pre + "r%d" % k, [last, "bias1"], lambda h=h, total=total: SC.activation(h, total, F.Relu, bias=T.bias1[:, 0:1], scale=0.25))
+                low = int(kind == "H")
+                for name in ORD["a%d" % s]:
+                    if name.startswith("%d." % k) and int(name[2]) >= low:
+                        d0, m = int(name[2]), len(name) - 2
+                        op(pre + name, start, lambda cc=cc, d0=d0, m=m, n=n, off=off: gather(
+                            "a", cgb[s][:, cc + d0 * n:cc + (d0 + m) * n], win[s][:], off(d0, m)))
+                        for d in range(d0, d0 + m):
+                            op(pre + "c%d.%d" % (k, d), [pre + name, ident], lambda cc=cc, d=d, n=n, total=total, ident=ident, low=low: PE.matmul(
+                                total, T[ident][:], cgb[s][:, cc + d * n:cc + (d + 1) * n], d == low, d == 3))
+                cc += 4 * n
+                if kind == "H":
+                    op(pre + "%d.0" % k, start, lambda a=a, off=off: gather("a", a, win[s][:], off(0), bias))
+                    op(pre + "r%d" % k, [pre + "c%d.3" % k, pre + "%d.0" % k], lambda a=a, total=total: V.tensor_tensor(a, total, a, A.add))
+                elif s == S - 1:
+                    op(pre + "r%d" % k, [pre + "c%d.3" % k, "bias1"], lambda h=h, total=total: SC.activation(
+                        h, total, F.Relu, bias=T.bias[:, 3:4], scale=last_scale))
                 elif rq == "a":
-                    op(pre + "r%d" % k, [last], lambda a=a, total=total: SC.activation(a, total, F.Identity, bias=bias))
+                    op(pre + "r%d" % k, [pre + "c%d.3" % k], lambda a=a, total=total: SC.activation(a, total, F.Relu, bias=bias))
                 else:
-                    op(pre + "r%d" % k, [last], lambda a=a, total=total: V.tensor_scalar(a, total, bias, None, A.add))
+                    op(pre + "r%d" % k, [pre + "c%d.3" % k], lambda a=a, total=total: V.tensor_scalar(a, total, bias, 0.0, A.add, A.max))
                 done.append(pre + "r%d" % k)
             else:
                 op(pre + "%d.0" % k, start, lambda a=a, off=off, kind=kind: gather("v" if kind == "D" else "a", a, win[s][:], off(0), bias))
@@ -251,73 +317,77 @@ def rank_program(g, core, T, topo):
                         a, win[s][:].indirect(off(d)), a, A.add))
                 done.append(pre + "%d.3" % k)
                 if s == S - 1:
-                    op(pre + "r%d" % k, [pre + "%d.3" % k], lambda h=h, a=a, rq=rq: finish(rq, h, a))
+                    op(pre + "r%d" % k, [pre + "%d.3" % k], lambda h=h, a=a, rq=rq: finish(rq, h, a, last_scale))
+                elif "r%d" % k in ORD["v%d" % s] + ORD["a%d" % s]:
+                    assert c0 == cut
+                    op(pre + "r%d" % k, [pre + "%d.3" % k], lambda a=a, rq=rq: finish(rq, a, a))
+                    done.append(pre + "r%d" % k)
+                    cut += n
             if s == S - 1:
-                bank = ps[att_banks[k]][:, 0:n]
-                col = 6 if tanhs[-1] == "t%d" % k else tanhs.index("t%d" % k)
+                bank = ps[ATT_BANKS[k]][:, 0:n]
+                col = tanhs.index("t%d" % k)
                 op(pre + "m%d" % k, [pre + "r%d" % k, "aw7"], lambda bank=bank, h=h: PE.matmul(bank, T.abd[:], h, True, True))
                 op(pre + "t%d" % k, [pre + "m%d" % k, "aw7"], lambda bank=bank, col=col, c0=c0, n=n: SC.activation(
                     T.tnh[:, c0:c0 + n], bank, F.Tanh, bias=T.abc[:, 0:1], accum_out=T.tsum[:, col:col + 1]))
             c0 += n
         for q in "vap":
-            put(q, *[pre + x for x in ORD["%s%d" % (q, s)]])
-        return done
+            put(q, *[pre + x if pre + x in ops else x for x in ORD["%s%d" % (q, s)]])
+        return done, (cut, sum(n for kind, n in CHUNKS[s] if kind != "C"))
 
-    put("g", "moi", "dif", "idn", "mpb", "sendq")
-    put("v", "ones", "mou", "difq", "abd0", "idb", "sndf", "perm0", "perm1", "snd0", "perm2")
-    put("p", "psnd0", *psm, "psrc0a", "psrc0")
-    slots(0, ["x0", "snd0"])
-    put("g", "pi", "blk")
-    put("v", "srcf0", "srcf1", "bias4", "bias1", "src0a", "src0", "snd12")
-    done = step(0)
+    for q in "gvap":
+        put(q, *START[q])
+    start = slots(0, ["x0", "snd0"], 0)
+    order["a"].insert(-1, "pm32")
+    put("a", "idb")
+    done, cut = step(0, start)
     put("p", "psrc1")
-    slots(1, done + ["snd12"])
-    put("v", "pg", "ownv1", "src1", "pgf", "aqs", "m16")
-    done = step(1)
+    start = slots(1, done + ["snd12"], cut)
+    put("a", "bias1")
+    done, cut = step(1, start)
     put("p", "psrc2")
-    slots(2, done)
-    put("v", "ownv2", "src2", "qm0", "qm1", "qm2", "qm3")
-    step(2)
+    step(2, slots(2, done, cut))
 
+    assert len(tanhs) == 7
     tl = "2:" + tanhs[-1]
-    op("tpart", ["2:" + x for x in tanhs[:-1]], lambda: V.tensor_reduce(T.tsum[:, 7:8], T.tsum[:, 0:len(tanhs) - 1], AxisListType.X, A.add))
-    remote("sends", ["tpart", tl], lambda: g.remote_dma_fused([RemoteDMATransfer(
-        dst_ids=[dst(q)], dma_engine_mask=small_masks[i], remote_sem=T.sem["arrf" if q in far else "arrn"],
-        src=T.tsum[:, 6:8], dst=T.sin[:, 2 * rank:2 * rank + 2]) for i, q in enumerate(peers)], local_sem=T.sem.sent))
+    op("tpart", ["2:" + x for x in tanhs[:-1]], lambda: V.tensor_reduce(T.tsum[:, 7:8], T.tsum[:, 0:6], AxisListType.X, A.add))
+    sums, land = T.tsum[:, 6:8], T.sin[:, 2 * rank:2 * rank + 2]
+    remote("sums0", ["tpart", tl], [(cores[far[0]], off_eng, "arrf0", sums, land), (cores[near[0]], on_eng, "arrn", sums, land)])
+    remote("sums1", [], [(cores[far[1]], off_eng, "arrf1", sums, land)])
 
-    def score(q, out, start, stop):
-        return PE.matmul(out, T.qm[:, 128 * q:128 * q + 128], T.tsum[:, 6:8] if q == rank else T.sin[:, 2 * q:2 * q + 2], start, stop)
-    op("sco", ["tpart", tl, "qm3", "src2"], lambda: score(rank, ps[4][:, 0:2], True, True))
-    op("scn", ["arrn"], lambda: score(near[0], ps[7][:, 0:2], True, False))
-    op("scf0", ["arrf"], lambda: score(far[0], ps[7][:, 0:2], False, False))
-    op("scf1", ["arrf"], lambda: score(far[1], ps[7][:, 0:2], False, True))
-    op("exo", ["sco"], lambda: SC.activation(T.exo[:, 0:2], ps[4][:, 0:2], F.Exp))
-    op("mx", ["exo", "m16"], lambda: V.tensor_scalar(T.mx[:], T.m16[:], T.exo[:, 0:1], T.exo[:, 1:2], A.mult, A.mult))
-    op("exr", ["scf1"], lambda: SC.activation(T.exr[:, 0:2], ps[7][:, 0:2], F.Exp))
+    def score(q, out, cols, start, stop):
+        return out, T.qm[:, 128 * q:128 * q + 128], cols, start, stop
+    rest = ps[7][:, 0:2]
+    first = ps[ATT_BANKS[int(tanhs[0][1:])]][:, 0:1]
+    matmuls("sc0", ["2:" + tanhs[0], "qm0"], [score(rank, first, T.tsum[:, 0:1], True, True)])
+    matmuls("sco", ["tpart", tl], [score(rank, rest, T.tsum[:, c:c + 2], c == 1, False) for c in (1, 3, 5)])
+    matmuls("scn", ["arrn", "qm3"], [score(near[0], rest, T.sin[:, 2 * near[0]:2 * near[0] + 2], False, False)])
+    matmuls("scf0", ["arrf0"], [score(far[0], rest, T.sin[:, 2 * far[0]:2 * far[0] + 2], False, False)])
+    matmuls("scf", ["arrf1"], [score(far[1], rest, T.sin[:, 2 * far[1]:2 * far[1] + 2], False, True)])
+    op("exo", ["sc0"], lambda: SC.activation(T.exo[:, 0:1], first, F.Exp, scale=2.0 ** -14))
+    op("mx", ["exo", "m16"], lambda: V.tensor_scalar(T.mx[:], T.m16[:], T.exo[:, 0:1], None, A.mult))
+    op("exr", ["scf"], lambda: SC.activation(T.exr[:, 0:2], rest, F.Exp, scale=2.0 ** -14))
     op("wm", ["mx", "exr"], lambda: V.tensor_scalar(T.wm[:], T.mx[:], T.exr[:, 0:1], T.exr[:, 1:2], A.mult, A.mult))
     dma("ow", "ow", ["wm"], lambda: SY.dma_start(T.w[:], T.wm[0:128:16, 0:1]))
-    put("p", "sco", "scn", "scf0", "scf1")
-    put("v", "tpart", "mx", "wm")
-    put("g", "sends")
+    put("p", "sc0", "sco", "scn", "scf0", "scf")
+    put("v", "tpart", "pg", "qm1", "pgf", "qm2", "m16", "qm3", "mx", "wm")
+    put("g", "sums0", "sums1")
     put("a", "exo", "exr")
     put("s", "ow")
 
-    for half in range(2):
-        names = []
-        for b in range(4 * half, 4 * half + 4):
-            for u in range(2):
-                names.append("y%d.%d" % (b, u))
-                op(names[-1], ["wm"], lambda half=half, b=b, u=u: PE.matmul(
-                    ps[half][:, 32 * (b % 4) + u:32 * (b % 4) + 32:2], T.hfin[:, 8 * u + b], T.wm[:], True, True))
-        op("yo%d" % half, names, lambda half=half: V.transpose(T.yo[:, 128 * half:128 * half + 128], ps[half][:, 0:128]))
-        put("p", *names)
-        put("v", "yo%d" % half)
-    for a in range(4):
-        dma("yd%d" % a, "oy", ["yo0", "yo1"], lambda a=a: (SY if a % 2 else SC).dma_start(
-            T.y[:, 512 * a:512 * a + 512], T.yo[32 * a:32 * a + 32, :]))
-        put("s" if a % 2 else "a", "yd%d" % a)
+    for i, (b0, b1) in enumerate(PARTS):
+        n = b1 - b0
+        matmuls("y%d" % i, ["wm"], [(ps[i][:, 32 * b + u:32 * b + 32:2], T.hfin[:, 2 * b0 + n * u + b], T.wm[:], True, True)
+                                    for b in range(n) for u in range(2)])
+        op("yo%d" % i, ["y%d" % i], lambda i=i, b0=b0, b1=b1, n=n: V.transpose(T.yo[:, 32 * b0:32 * b1], ps[i][:, 0:32 * n]))
+        put("p", "y%d" % i)
+        put("v", "yo%d" % i)
+        for a in range(4):
+            dma("yd%d.%d" % (i, a), "oy", ["yo%d" % i], lambda a=a, b0=b0, b1=b1: (SY if a % 2 else SC).dma_start(
+                T.y[:, 512 * a + 64 * b0:512 * a + 64 * b1], T.yo[32 * a:32 * a + 32, 32 * b0:32 * b1]))
+            put("s" if a % 2 else "a", "yd%d.%d" % (i, a))
 
     total = dict(dmas)
+    total["sent"] = tok["sent"][1]
     for q, names in order.items():
         n = 0
         for name in names:
@@ -346,7 +416,6 @@ def rank_program(g, core, T, topo):
                 ins.then_inc(T.sem["c" + q], 1)
             elif kind != "remote":
                 ins.then_inc(T.sem[kind], 16)
-    total["sent"] = S * n_slots + 2 * n_small
     for sem, val in total.items():
         if max(seen.get((q, sem), 0) for q in eng) < val:
             g.wait_ge(T.sem[sem], val)

from concourse.bass import DstId, RemoteDMATransfer
from concourse.mybir import AluOpType, AxisListType, ActivationFunctionType

E, CAP, P, S = 2048, 512, 4096, 3
F32, BF, F16, I32, U16 = "float32", "bfloat16", "float16", "int32", "uint16"

SCRATCH = {
    "win0": ("sbuf", [128, P], BF), "win1": ("sbuf", [128, P], F32), "win2": ("sbuf", [128, P], F32),
    "hfin": ("sbuf", [128, 16, 4, 32], F32),
    "sb0": ("sbuf", [128, 3 * CAP], BF), "sb1": ("sbuf", [128, 3 * CAP], F32), "sb2": ("sbuf", [128, 3 * CAP], F32),
    "acc2": ("sbuf", [128, E], F32),
    "cg0": ("sbuf", [128, 4 * 768], BF), "cg1": ("sbuf", [128, 4 * 768], F32), "cg2": ("sbuf", [128, 4 * 768], F32),
    "srci": ("sbuf", [128, 4, 128], I32), "sndi": ("sbuf", [128, 128], I32),
    "srcf": ("sbuf", [128, 4, 128], F16), "sndf": ("sbuf", [128, 128], F16),
    "src0": ("sbuf", [128, 512], U16), "src1": ("sbuf", [128, 512], U16), "src2": ("sbuf", [128, 512], U16),
    "snd0": ("sbuf", [128, 128], U16), "snd12": ("sbuf", [128, 256], U16),
    "bsb": ("sbuf", [128, 4], F32), "bias": ("sbuf", [128, 4], F32), "bsc": ("sbuf", [128, 4], F32),
    "mp1": ("sbuf", [1, 24], I32), "mpb": ("sbuf", [128, 24], I32),
    "moi": ("sbuf", [128, 24], I32), "mou": ("sbuf", [128, 24], U16),
    "dif": ("sbuf", [128, 128], F32), "difq": ("sbuf", [128, 128], F32),
    "pmat": ("sbuf", [128, 384], BF), "pm32": ("sbuf", [128, 384], F32),
    "ones": ("sbuf", [128, 128], F32), "idn": ("sbuf", [128, 128], F32), "idb": ("sbuf", [128, 128], BF),
    "pi": ("sbuf", [128, 4], I32), "pg": ("sbuf", [128, 4], I32), "pgf": ("sbuf", [128, 4], F32),
    "blk": ("sbuf", [128, 24], F32), "qm": ("sbuf", [128, 512], F32), "m16": ("sbuf", [128, 16], F32),
    "abd": ("sbuf", [128, 128], F32), "abc": ("sbuf", [128, 4], F32), "aqc": ("sbuf", [128, 4], F32),
    "aqd": ("dram", [128, 2], F32), "aqin": ("dram", [4, 128, 2], F32),
    "tnh": ("sbuf", [128, E], F32), "tsum": ("sbuf", [128, 8], F32),
    "sin": ("sbuf", [128, 8], F32), "exo": ("sbuf", [128, 4], F32), "exr": ("sbuf", [128, 4], F32),
    "mx": ("sbuf", [128, 16], F32), "wm": ("sbuf", [128, 16], F32),
    "yo": ("sbuf", [128, 256], F32),
}
for _b in range(8):
    SCRATCH["ps%d" % _b] = ("psum", [128, 512], F32)

SEMAPHORES = ["cv", "ca", "cp", "cg", "lx", "lsnd", "lsrc", "lmp", "lbs", "lpar", "laq", "sent",
              "arr0", "arr1", "arr2", "relq", "rel0_0", "rel0_1", "rel1_0", "rel1_1", "rel2_0", "rel2_1", "arrq", "arrn", "arrf0", "arrf1", "ow", "oy"]

CHUNKS = [
    [("D", 288), ("A", 128), ("A", 928), ("C", 416), ("C", 288)],
    [("D", 256), ("A", 128), ("A", 480), ("A", 448), ("H", 480), ("H", 256)],
    [("D", 384), ("A", 128), ("A", 224), ("A", 288), ("A", 512), ("A", 96), ("C", 416)],
]
ORD = {
    "v0": "0.0 1.1 0.1 1.2 0.2 2.1 0.3 2.2 1.3 2.3".split(),
    "a0": "1.0 2.0 3.0123 4.012 4.3 r3 r4".split(),
    "p0": "c3.0 c3.1 c3.2 c3.3 c4.0 c4.1 c4.2 c4.3".split(),
    "v1": "0.0 1.1 0.1 1.2 0.2 1.3 2.1 0.3 2.2 3.1 2.3 3.2 r4 3.3 r5".split(),
    "a1": "1.0 4.1 2.0 5.1 4.2 3.0 4.3 5.2 4.0 5.3 5.0 r0 r1 qm0".split(),
    "p1": "c4.1 c5.1 c4.2 c4.3 c5.2 c5.3".split(),
    "v2": "0.0 0.1 2.1 0.2 2.2 0.3 4.1 2.3 4.2 3.1 4.3 3.2 1.1 3.3 5.1 1.2 5.2 1.3 5.3 r1 r5".split(),
    "a2": "6.0 2.0 6.1 6.2 4.0 6.3 3.0 r0 r2 5.0 1.0 r6 r4 t2 t0 r3 t6 t4 t3 t1 t5".split(),
    "p2": "c6.0 c6.1 c6.2 c6.3 m0 m2 m6 m4 m3 m1 m5".split(),
}
ATT_BANKS = [1, 5, 0, 4, 3, 6, 2]
SLOTS = [("v", 0, 0, 128), ("a", 1, 256, 384), ("v", 0, 128, 256), ("a", 1, 384, 512), ("v", 0, 256, 512), ("a", 2, 0, 256),
         ("v", 1, 0, 256), ("a", 2, 256, 512), ("v", None, 0, 192), ("a", None, 192, 512)]
CALLS = [[(0, 0, 128), ("h", 256, 384)], [(0, 128, 256), ("h", 384, 512)], [(0, 256, 512), (2, 0, 256)], [(1, 0, 256), (2, 256, 512)]]
SLOTS0 = [("v", 0, 0, 256), ("a", 0, 256, 512), ("v", 1, 0, 512), ("a", 2, 0, 512), ("a", None, 0, 512)]
CALLS0 = [[(0, 0, 512)], [(1, 0, 512), (2, 0, 512)]]
FINISH_V = [576, 672]
START = {
    "g": "blk0 moi dif mpb sendq pi idn".split(),
    "v": "ones bsc abd0 mou difq sndf perm0 perm1 snd0 perm2".split(),
    "a": "blk1 blk".split(),
    "p": "psnd0 psn psrc0 pb".split(),
}
FILL = ["srcf snd12 src0 bias".split(), ["src1"], ["src2"]]
PARTS = [(0, 4), (4, 8)]


def rank_program(g, core, T, topo):
    cores = list(T.cores)

    def places(rank):
        me = cores[rank]
        near = [q for q in range(len(cores)) if q != rank and topo.chip(cores[q]) == topo.chip(me)]
        far = [q for q in range(len(cores)) if topo.chip(cores[q]) != topo.chip(me)]
        far.sort(key=lambda q: topo.die(cores[q]) == topo.die(me))
        helper = [c for c in topo.cores_of(me) if c not in cores and topo.die(c) == topo.die(me) and topo.may_write(c, cores[far[-1]])]
        return far, near, helper[0]

    def write(parts):
        return g.remote_dma_fused([RemoteDMATransfer(
            dst_ids=[DstId(rid=topo.addr(c)[0], pnc=topo.addr(c)[1])], dma_engine_mask=sum(1 << e for e in engines),
            remote_sem=T.sem[sem], src=src, dst=land) for c, engines, sem, src, land in parts], local_sem=T.sem.sent)

    relayed = [[(a, b) for call in (CALLS if s else CALLS0) for blk, a, b in call if blk == "h"] for s in range(S)]
    rank = T.rank_of(core)
    if rank is None:
        for r in range(len(cores)):
            far, near, helper = places(r)
            if helper == core:
                to = cores[far[-1]]
                out = topo.engines(core, to)
                n_in = len([e for e in topo.engines(cores[r], core) if e not in out])
                g.wait_ge(T.sem.relq, n_in // 2)
                write([(to, out, "arrq", T.aqd[:], T.aqin[r])])
                for s in range(S):
                    for i, (a, b) in enumerate(relayed[s]):
                        g.wait_ge(T.sem["rel%d_%d" % (s, i)], n_in)
                        write([(to, out, "arr%d" % s, T["sb%d" % s][:, a:b], T["win%d" % s][:, E + CAP * r + a:E + CAP * r + b])])
                g.wait_ge(T.sem.sent, len(out) * (1 + sum(len(pieces) for pieces in relayed)))
        return
    A, F = AluOpType, ActivationFunctionType
    V, SC, PE, SY = g.vector, g.scalar, g.tensor, g.sync
    eng = {"v": V, "a": SC, "p": PE, "g": g, "s": SY}
    far, near, helper = places(rank)
    peers = far + near
    off_eng = topo.engines(core, cores[far[0]])
    on_eng = [e for e in topo.engines(core, cores[near[0]]) if e not in off_eng]
    block_eng = [off_eng] * len(far) + [on_eng]

    ops, order = {}, {q: [] for q in eng}
    tok, dmas, many = {}, {}, {}

    def op(name, deps, fn):
        ops[name] = (deps, fn, None)

    def dma(name, sem, deps, fn):
        ops[name] = (deps, fn, sem)
        dmas[sem] = dmas.get(sem, 0) + 16

    def remote(name, deps, parts):
        ops[name] = (deps, lambda: write([part[:5] for part in parts]), "remote")
        for part in parts:
            for s, n in (("sent", len(part[1])), (part[5], len(off_eng)) if part[0] == helper else (part[2], len(part[1]))):
                tok[s] = (s, tok.get(s, (s, 0))[1] + n)

    def put(q, *names):
        for name in names:
            order[q].extend(many.get(name, [name]))

    def matmuls(name, deps, calls):
        many[name] = ["%s#%d" % (name, i) for i in range(len(calls) - 1)] + [name]
        for nm, c in zip(many[name], calls):
            op(nm, deps, lambda c=c: PE.matmul(*c))

    def gather(q, out, win, off, bias=None, relu=False):
        src = win.indirect(off)
        if relu:
            return finish(q, out, src)
        if q == "a":
            if bias is None:
                return SC.activation(out, src, F.Copy)
            return SC.activation(out, src, F.Identity, bias=bias)
        if bias is None:
            return V.tensor_copy(out, src)
        return V.tensor_scalar(out, src, bias, None, A.add)

    def finish(q, out, total, scale=1.0):
        if q == "a":
            return SC.activation(out, total, F.Relu, scale=scale)
        return V.tensor_scalar(out, total, scale, 0.0, A.mult, A.max)

    ps = [T["ps%d" % b] for b in range(8)]
    win = [T.win0, T.win1, T.win2]
    sb = [T.sb0, T.sb1, T.sb2]
    srcu = [T.src0, T.src1, T.src2]
    acc = [T.win1, T.win2, T.acc2]
    cgb = [T.cg0, T.cg1, T.cg2]
    last_scale = 0.25 ** S

    for k in range(8):
        dma("x%d" % k, "lx", [], lambda k=k, q=(SY if k < 4 else SC): q.dma_start(T.win0[16 * k:16 * k + 16, 0:E], T.x[:]))
    dma("snd", "lsnd", [], lambda: SY.dma_start(T.sndi[:], T.snd[:]))
    dma("mp", "lmp", [], lambda: SC.dma_start(T.mp1[:], T.mp[:]))
    dma("src", "lsrc", [], lambda: SY.dma_start(T.srci[:], T.src[:]))
    dma("bs", "lbs", [], lambda: SC.dma_start(T.bsb[:, 0:1], T.bs[:]))
    dma("aqd", "laq", [], lambda: SY.dma_start(T.aqd[0:8, :], T.aq[:]))
    dma("aqf", "laq", [], lambda: SC.dma_start(T.aqd[8:128, :], T.aw[0:15, :]))
    put("s", "aqd", "snd", "x0", "x1", "x2", "x3", "src")
    put("a", "mp", "aqf", "x4", "x5", "x6", "x7", "bs")
    for k in range(8):
        r = slice(16 * k, 16 * k + 16)
        dma("aw%d" % k, "lpar", ["arr0", "abd0"], lambda r=r: SY.dma_start(T.abd[r, r], T.aw[:]))
        dma("ab%d" % k, "lpar", [], lambda r=r: SY.dma_start(T.abc[r, 0:1], T.ab[:]))
        put("s", "aw%d" % k, "ab%d" % k)
        for q in range(len(cores)):
            dma("aq%d.%d" % (k, q), "lpar", ["arrq"], lambda r=r, q=q: SY.dma_start(
                T.aqc[r, q:q + 1], T.aq[:] if q == rank else T.aqin[q, 0:8, :]))
            put("s", "aq%d.%d" % (k, q))
    half_on = len(on_eng) // 2
    remote("sendq", ["aqd"], [(cores[far[0]], off_eng, "arrq", T.aqd[:], T.aqin[rank]),
                              (cores[near[0]], on_eng[:half_on], "arrq", T.aqd[:], T.aqin[rank]),
                              (helper, on_eng[half_on:], "relq", T.aqd[:], T.aqd[:], "arrq")])

    op("moi", [], lambda: g.iota(T.moi[:], [[1, 3], [3, 8]], 0, 0))
    op("dif", [], lambda: g.iota(T.dif[:], [[0, 8], [-1, 16]], 0, 1, allow_small_or_imprecise_dtypes=True))
    op("mpb", ["mp"], lambda: g.partition_broadcast(T.mpb[:], T.mp1[:], 128))
    op("pi", [], lambda: g.iota(T.pi[:, 0:1], [[1, 1]], 0, 1))
    op("idn", ["ones"], lambda: g.affine_select(T.idn[:], T.ones[:], [[-1, 128]], A.is_equal, 0.0, 0, 1))
    op("blk0", [], lambda: g.iota(T.blk[:], [[-32, 8], [0, S]], -15, 2, allow_small_or_imprecise_dtypes=True))
    op("blk1", ["blk0"], lambda: SC.activation(T.blk[:], T.blk[:], F.Square))
    op("blk", ["blk1", "bsc"], lambda: SC.activation(T.blk[:], T.blk[:], F.Tanh, bias=T.bsc[:, 3:4], scale=-1.0))
    op("abd0", [], lambda: V.memset(T.abd[:], 0.0))
    op("ones", [], lambda: V.memset(T.ones[:], 1.0))
    many["bsc"] = ["bsc0", "bsc1", "bsc2", "bsc"]
    for i, (name, val) in enumerate(zip(many["bsc"], (4.0, 16.0, 64.0, 257.0))):
        op(name, [], lambda i=i, val=val: V.memset(T.bsc[:, i:i + 1], val))
    op("idb", ["idn"], lambda: SC.activation(T.idb[:], T.idn[:], F.Copy))
    op("mou", ["moi"], lambda: V.tensor_copy(T.mou[:], T.moi[:]))
    op("difq", ["dif"], lambda: V.tensor_scalar(T.difq[:], T.dif[:], 1.0 / 16, None, A.mult))
    op("sndf", ["snd"], lambda: V.tensor_copy(T.sndf[:], T.sndi[:]))
    op("srcf", ["src"], lambda: V.tensor_scalar(T.srcf[:], T.srci[:], -float(E), None, A.add))

    def perm(s, m=T.pmat):
        return m[:, 128 * s:128 * s + 128]
    for s in range(S):
        op("perm%d" % s, ["mpb", "mou", "difq"], lambda s=s: V.tensor_tensor(
            perm(s), T.mpb[:, 0:24].indirect(T.mou[:, 8 * s:8 * s + 8]), T.difq[:], A.is_equal))
    op("pm32", ["perm0", "perm1", "perm2"], lambda: SC.activation(T.pm32[:], T.pmat[:], F.Copy))
    for s in range(S):
        calls, c0 = [], 0
        for kind, n in CHUNKS[s]:
            calls.append((ps[4][:, c0 // 4:(c0 + n) // 4], perm(s), T.srcf[:, :, c0 // 16:(c0 + n) // 16], True, True))
            c0 += n
        matmuls("psrc%d" % s, ["perm%d" % s, "srcf"] + (["src%d" % (s - 1)] if s else []), calls)
        op("src%d" % s, ["psrc%d" % s], lambda s=s: V.tensor_scalar(srcu[s][:], ps[4][:], float(E), None, A.add))
    op("psnd0", ["perm0", "sndf"], lambda: PE.matmul(ps[5][:, 0:128], perm(0), T.sndf[:], True, True))
    op("snd0", ["psnd0"], lambda: V.tensor_copy(T.snd0[:], ps[5][:, 0:128]))
    matmuls("pb", ["pm32", "bs", "snd0"], [(ps[5][:, 256 + s:257 + s], perm(s, T.pm32), T.bsb[:, 0:1], True, True) for s in range(S)])
    matmuls("psn", ["perm1", "perm2", "sndf"], [(ps[6][:, 128 * (s - 1):128 * s], perm(s), T.sndf[:], True, True) for s in (1, 2)])
    op("bias1", ["bias"], lambda: SC.activation(T.bias[:, 3:4], ps[5][:, 258:259], F.Copy))
    op("bias", ["pb", "bsc"], lambda: V.tensor_tensor(T.bias[:, 0:3], ps[5][:, 256:259], T.bsc[:, 0:3], A.mult))
    op("snd12", ["psn"], lambda: V.tensor_copy(T.snd12[:], ps[6][:, 0:256]))
    op("pg", ["pi"], lambda: V.tensor_scalar(T.pg[:, 0:1], T.pi[:, 0:1], 4, None, A.arith_shift_right))
    op("pgf", ["pg"], lambda: V.tensor_copy(T.pgf[:, 0:1], T.pg[:, 0:1]))
    op("m16", ["pgf", "difq"], lambda: V.tensor_scalar(T.m16[:], T.difq[:, 0:16], T.pgf[:, 0:1], None, A.is_equal))
    for i, q in enumerate([rank] + near + far):
        out, aq = T.qm[:, 128 * q:128 * q + 128], T.aqc[:, q:q + 1]
        wide = T.blk[:].indirect(T.mou[:, 0:8])
        if "qm%d" % i in ORD["a1"]:
            op("qm%d" % i, ["blk", "mou", "aw7"], lambda out=out, aq=aq, wide=wide: SC.activation(out, wide, F.Identity, bias=aq, scale=aq))
        else:
            op("qm%d" % i, ["blk", "mou", "aw7"], lambda out=out, aq=aq, wide=wide: V.tensor_scalar(out, wide, 1.0, aq, A.add, A.mult))

    def slots(s, ready, cut):
        lst, base = (T.snd0, 0) if s == 0 else (T.snd12, 128 * (s - 1))
        at = E + CAP * rank
        names = []
        for i, (q, blk, a, b) in enumerate(SLOTS if s else SLOTS0):
            to = rank if blk is None else peers[blk]
            out = win[s][:, at + a:at + b] if blk is None else sb[s][:, CAP * blk + a:CAP * blk + b]
            off = lst[:, base + 32 * to + a // 16:base + 32 * to + b // 16]
            names.append("g%d.%d" % (s, i))
            op(names[-1], ready, lambda q=q, out=out, off=off: gather(q, out, win[s][:, 0:E], off, relu=s > 0))
            put(q, names[-1])
        for i, call in enumerate(CALLS if s else CALLS0):
            deps, parts = [], []
            for via, a, b in call:
                blk = len(far) - 1 if via == "h" else via
                deps += [names[k] for k, (q, blk2, a2, b2) in enumerate(SLOTS if s else SLOTS0) if blk == blk2 and a < b2 and a2 < b]
                src = sb[s][:, CAP * blk + a:CAP * blk + b]
                if via == "h":
                    parts.append((helper, on_eng, "rel%d_%d" % (s, relayed[s].index((a, b))), src, sb[s][:, a:b], "arr%d" % s))
                else:
                    engines = block_eng[blk]
                    alike = [piece for piece in call if piece[0] != "h" and block_eng[piece[0]] == engines]
                    n = len(engines) // len(alike)
                    k = alike.index((via, a, b))
                    parts.append((cores[peers[blk]], engines[k * n:(k + 1) * n], "arr%d" % s, src, win[s][:, at + a:at + b]))
            remote("send%d.%d" % (s, i), deps, parts)
            put("g", "send%d.%d" % (s, i))
        put("v", *FILL[s][:1])
        if s:
            mid = cut[0] + FINISH_V[s - 1]
            for q, a, b in (("v", cut[0], mid), ("a", mid, cut[1])):
                op("own%s%d" % (q, s), names, lambda q=q, a=a, b=b: finish(q, win[s][:, a:b], win[s][:, a:b]))
                put(q, "own%s%d" % (q, s))
            names = names + ["ownv%d" % s, "owna%d" % s]
        put("v", *FILL[s][1:])
        return names + ["arr%d" % s, "src%d" % s, "bias"]

    tanhs = [x for x in ORD["a2"] if x[0] == "t"]

    def step(s, start):
        pre = "%d:" % s
        bias = T.bias[:, s:s + 1]
        c0 = cc = cut = 0
        cbanks = [7, 3]
        done = []
        for k, (kind, n) in enumerate(CHUNKS[s]):
            def off(d, m=1, c0=c0, n=n):
                at = c0 // 4 + d * n // 16
                return srcu[s][:, at:at + m * n // 16]
            rq = "v" if "r%d" % k in ORD["v%d" % s] else "a"
            a = acc[s][:, c0:c0 + n]
            h = T.hfin[:, c0 % 512 // 32:(c0 % 512 + n) // 32, c0 // 512, :] if s == S - 1 else None
            if kind in "CH":
                total = ps[cbanks.pop(0)][:, 0:n]
                ident = "idb" if s == 0 else "idn"
                low = int(kind == "H")
                for name in ORD["a%d" % s]:
                    if name.startswith("%d." % k) and int(name[2]) >= low:
                        d0, m = int(name[2]), len(name) - 2
                        op(pre + name, start, lambda cc=cc, d0=d0, m=m, n=n, off=off: gather(
                            "a", cgb[s][:, cc + d0 * n:cc + (d0 + m) * n], win[s][:], off(d0, m)))
                        for d in range(d0, d0 + m):
                            op(pre + "c%d.%d" % (k, d), [pre + name, ident], lambda cc=cc, d=d, n=n, total=total, ident=ident, low=low: PE.matmul(
                                total, T[ident][:], cgb[s][:, cc + d * n:cc + (d + 1) * n], d == low, d == 3))
                cc += 4 * n
                if kind == "H":
                    op(pre + "%d.0" % k, start, lambda a=a, off=off: gather("a", a, win[s][:], off(0), bias))
                    op(pre + "r%d" % k, [pre + "c%d.3" % k, pre + "%d.0" % k], lambda a=a, total=total: V.tensor_tensor(a, total, a, A.add))
                elif s == S - 1:
                    op(pre + "r%d" % k, [pre + "c%d.3" % k, "bias1"], lambda h=h, total=total: SC.activation(
                        h, total, F.Relu, bias=T.bias[:, 3:4], scale=last_scale))
                elif rq == "a":
                    op(pre + "r%d" % k, [pre + "c%d.3" % k], lambda a=a, total=total: SC.activation(a, total, F.Relu, bias=bias))
                else:
                    op(pre + "r%d" % k, [pre + "c%d.3" % k], lambda a=a, total=total: V.tensor_scalar(a, total, bias, 0.0, A.add, A.max))
                done.append(pre + "r%d" % k)
            else:
                op(pre + "%d.0" % k, start, lambda a=a, off=off, kind=kind: gather("v" if kind == "D" else "a", a, win[s][:], off(0), bias))
                for d in (1, 2, 3):
                    op(pre + "%d.%d" % (k, d), start + [pre + "%d.%d" % (k, d - 1)], lambda a=a, d=d, off=off: V.tensor_tensor(
                        a, win[s][:].indirect(off(d)), a, A.add))
                done.append(pre + "%d.3" % k)
                if s == S - 1:
                    op(pre + "r%d" % k, [pre + "%d.3" % k], lambda h=h, a=a, rq=rq: finish(rq, h, a, last_scale))
                elif "r%d" % k in ORD["v%d" % s] + ORD["a%d" % s]:
                    assert c0 == cut
                    op(pre + "r%d" % k, [pre + "%d.3" % k], lambda a=a, rq=rq: finish(rq, a, a))
                    done.append(pre + "r%d" % k)
                    cut += n
            if s == S - 1:
                bank = ps[ATT_BANKS[k]][:, 0:n]
                col = tanhs.index("t%d" % k)
                op(pre + "m%d" % k, [pre + "r%d" % k, "aw7"], lambda bank=bank, h=h: PE.matmul(bank, T.abd[:], h, True, True))
                op(pre + "t%d" % k, [pre + "m%d" % k, "aw7"], lambda bank=bank, col=col, c0=c0, n=n: SC.activation(
                    T.tnh[:, c0:c0 + n], bank, F.Tanh, bias=T.abc[:, 0:1], accum_out=T.tsum[:, col:col + 1]))
            c0 += n
        for q in "vap":
            put(q, *[pre + x if pre + x in ops else x for x in ORD["%s%d" % (q, s)]])
        return done, (cut, sum(n for kind, n in CHUNKS[s] if kind != "C"))

    for q in "gvap":
        put(q, *START[q])
    start = slots(0, ["x0", "snd0"], 0)
    order["a"].insert(-1, "pm32")
    put("a", "idb")
    done, cut = step(0, start)
    put("p", "psrc1")
    start = slots(1, done + ["snd12"], cut)
    put("a", "bias1")
    done, cut = step(1, start)
    put("p", "psrc2")
    step(2, slots(2, done, cut))

    assert len(tanhs) == 7
    tl = "2:" + tanhs[-1]
    op("tpart", ["2:" + x for x in tanhs[:-1]], lambda: V.tensor_reduce(T.tsum[:, 7:8], T.tsum[:, 0:6], AxisListType.X, A.add))
    sums, land = T.tsum[:, 6:8], T.sin[:, 2 * rank:2 * rank + 2]
    remote("sums0", ["tpart", tl], [(cores[far[0]], off_eng, "arrf0", sums, land), (cores[near[0]], on_eng, "arrn", sums, land)])
    remote("sums1", [], [(cores[far[1]], off_eng, "arrf1", sums, land)])

    def score(q, out, cols, start, stop):
        return out, T.qm[:, 128 * q:128 * q + 128], cols, start, stop
    rest = ps[7][:, 0:2]
    first = ps[ATT_BANKS[int(tanhs[0][1:])]][:, 0:1]
    matmuls("sc0", ["2:" + tanhs[0], "qm0"], [score(rank, first, T.tsum[:, 0:1], True, True)])
    matmuls("sco", ["tpart", tl], [score(rank, rest, T.tsum[:, c:c + 2], c == 1, False) for c in (1, 3, 5)])
    matmuls("scn", ["arrn", "qm3"], [score(near[0], rest, T.sin[:, 2 * near[0]:2 * near[0] + 2], False, False)])
    matmuls("scf0", ["arrf0"], [score(far[0], rest, T.sin[:, 2 * far[0]:2 * far[0] + 2], False, False)])
    matmuls("scf", ["arrf1"], [score(far[1], rest, T.sin[:, 2 * far[1]:2 * far[1] + 2], False, True)])
    op("exo", ["sc0"], lambda: SC.activation(T.exo[:, 0:1], first, F.Exp, scale=2.0 ** -14))
    op("mx", ["exo", "m16"], lambda: V.tensor_scalar(T.mx[:], T.m16[:], T.exo[:, 0:1], None, A.mult))
    op("exr", ["scf"], lambda: SC.activation(T.exr[:, 0:2], rest, F.Exp, scale=2.0 ** -14))
    op("wm", ["mx", "exr"], lambda: V.tensor_scalar(T.wm[:], T.mx[:], T.exr[:, 0:1], T.exr[:, 1:2], A.mult, A.mult))
    dma("ow", "ow", ["wm"], lambda: SY.dma_start(T.w[:], T.wm[0:128:16, 0:1]))
    put("p", "sc0", "sco", "scn", "scf0", "scf")
    put("v", "tpart", "pg", "qm1", "pgf", "qm2", "m16", "qm3", "mx", "wm")
    put("g", "sums0", "sums1")
    put("a", "exo", "exr")
    put("s", "ow")

    for i, (b0, b1) in enumerate(PARTS):
        n = b1 - b0
        matmuls("y%d" % i, ["wm"], [(ps[i][:, 32 * b + u:32 * b + 32:2], T.hfin[:, 2 * b0 + n * u + b], T.wm[:], True, True)
                                    for b in range(n) for u in range(2)])
        op("yo%d" % i, ["y%d" % i], lambda i=i, b0=b0, b1=b1, n=n: V.transpose(T.yo[:, 32 * b0:32 * b1], ps[i][:, 0:32 * n]))
        put("p", "y%d" % i)
        put("v", "yo%d" % i)
        for a in range(4):
            dma("yd%d.%d" % (i, a), "oy", ["yo%d" % i], lambda a=a, b0=b0, b1=b1: (SY if a % 2 else SC).dma_start(
                T.y[:, 512 * a + 64 * b0:512 * a + 64 * b1], T.yo[32 * a:32 * a + 32, 32 * b0:32 * b1]))
            put("s" if a % 2 else "a", "yd%d.%d" % (i, a))

    total = dict(dmas)
    total["sent"] = tok["sent"][1]
    for q, names in order.items():
        n = 0
        for name in names:
            kind = ops[name][2]
            if kind is None:
                n += 1
                tok[name] = ("c" + q, n)
            elif kind != "remote":
                tok[name] = (kind, dmas[kind])
        if q != "s":
            total["c" + q] = n
    seen = {}
    for q, names in order.items():
        for name in names:
            deps, fn, kind = ops[name]
            want = {}
            for dname in deps:
                sem, val = tok[dname]
                want[sem] = max(want.get(sem, 0), val)
            for sem, val in want.items():
                if seen.get((q, sem), 0) < val:
                    eng[q].wait_ge(T.sem[sem], val)
                    seen[(q, sem)] = val
            ins = fn()
            if kind is None:
                ins.then_inc(T.sem["c" + q], 1)
            elif kind != "remote":
                ins.then_inc(T.sem[kind], 16)
    for sem, val in total.items():
        if max(seen.get((q, sem), 0) for q in eng) < val:
            g.wait_ge(T.sem[sem], val)
